import numpy as np, ml_dtypes
CORES = [51,54,179,182]
N = 4
BF = ml_dtypes.bfloat16
def gentries(a):
    return np.ascontiguousarray(a.reshape(8, 16, -1).transpose(0, 2, 1)).reshape(8, -1)
def gtable(e):
    e = np.asarray(e); return np.ascontiguousarray(e.reshape(8, -1, 16).transpose(0, 2, 1)).reshape(128, -1).astype(np.int32)
R, M, L, F, RO = 256, 256, 4, 256, 3
V = R + L * M
AT = [0] + [R + i * M for i in range(L + 1)]
LEV = np.repeat(np.arange(L + 1), np.diff(AT))
TOP = np.concatenate([2 * np.array(AT)[LEV[R:]], np.full(R, 2 * V)])
LOW = np.array(AT)[LEV + 1]
def under(rng, shape, top):
    return np.minimum((rng.random(shape) * top).astype(np.int64), np.asarray(top) - 1)
def parts(rng):
    i = np.arange(16)[:, None]; sh = (N, 8, 1, V)
    p = rng.integers(0, 16, sh); p2 = (p + rng.integers(1, 16, sh)) % 16
    t = 1 + (255 * rng.random(sh) ** (1.5 + LEV)).astype(np.int64); t2 = 1 + (255 * rng.random(sh) ** (1.5 + LEV)).astype(np.int64)
    x = np.where(i == p, t, 0); x = np.where((i == p2) & (rng.random(sh) < 0.125), t2, x); x = np.where(rng.random(sh) < 0.02, 0, x)
    s = (256 * rng.random((N, 8, 16, R)) ** 1.5).astype(np.int64)
    c = rng.integers(0, 256, (N, 8, 16, R + F)) * (rng.random((N, 8, 16, R + F)) > 0.15)
    half = rng.random(sh) < 0.75
    o = np.argsort(rng.random((N, 8, 16, V)) + 10 * (half & (i >= 8)), axis=2)
    k = np.where(half, rng.choice(np.array([0, 1, 1, 2, 2, 3, 4, 8]), sh), rng.choice(np.array([1, 2, 3, 5, 12, 16]), sh))
    e = np.where(o < k, under(rng, (N, 8, 16, V), TOP), 2 * V)
    a = LOW + under(rng, (N, 8, 2, V), V + R + F - LOW)
    return x, s, c[..., :R].copy(), c[..., R:].copy(), e, a
def rich(rng, x, v):
    k = rng.integers(3, 17, (N, 8, 1, V)); o = np.argsort(rng.random(x.shape), axis=2)
    return np.where(rng.random((N, 8, 1, V)) < 0.25, np.where(o < k, v, 0), x)
def pack(x, s, q, c, e, a):
    def b(v):
        return np.ascontiguousarray(v.reshape(N, 128, -1)).astype(np.float32).astype(BF)
    return {"piv": b(x), "safe": b(s), "lem": b(q), "leaf": b(c), "uses": np.ascontiguousarray(e.reshape(N, 128, V)).astype(np.int32), "prem": np.stack([gtable(v) for v in a.reshape(N, 8, 2 * V)])}
def setup_inputs(rng):
    return pack(*parts(rng))
def setup_inputs_turn(rng):
    x, s, q, c, e, a = parts(rng); i = np.arange(16)[:, None]
    j = rng.integers(0, 16, (N, 8, 1, 1)); w = rng.integers(0, 7, (N, 8, 1, V))
    w[..., :7] = np.arange(7)
    one, two = i == j, i == (j + 8) % 16
    m = np.where(w == 0, one, np.where(w == 1, two, np.where(w == 2, one | two, np.where(w == 3, i < 8, np.where(w == 4, i >= 8, w == 5)))))
    n = under(rng, (N, 8, 16, V), TOP); n = n - (n & 1) * (rng.random(n.shape) < 0.5)
    x = np.where(rng.random((N, 8, 1, V)) < 0.3, 0, x)
    return pack(x, s, q, c, np.where(m, n, 2 * V), a)
def setup_inputs_ties(rng):
    x, s, q, c, e, a = parts(rng); v = np.array([0, 1, 127, 128, 129, 254, 255])
    x = rich(rng, x, 1)
    x = np.where(x > 0, rng.choice(np.array([1, 127, 128, 129, 255]), x.shape), 0); nx = np.roll(x, 8, axis=2)
    s, q, c = rng.choice(v, s.shape), rng.choice(v, q.shape), rng.choice(v, c.shape)
    s[..., 0] = x[..., 0]; s[..., 1] = np.maximum(x[..., 1] - 1, 0); s[..., 2] = np.maximum(x[..., 2], nx[..., 2]); s[..., 3] = nx[..., 3]
    return pack(x, s, q, c, e, a)
def setup_inputs_alike(rng):
    x, s, q, c, e, a = parts(rng); on = e < 2 * V
    e[:, 1] = np.where(on[:, 1], under(rng, (N, 1, V), TOP), 2 * V)
    e[:, 2] = np.where(on[:, 2], np.where(rng.random((N, 16, V)) < 0.5, 0, TOP - 1), 2 * V)
    e[:, 3] = 2 * V
    e[:, 4] = np.where(on[:, 4], TOP - 1 - rng.integers(0, 16, (N, 16, V)), 2 * V)
    e[:, 5] = under(rng, (N, 16, V), TOP)
    a[:, 1, 1] = a[:, 1, 0]; a[:, 2] = np.where(rng.random((N, 2, V)) < 0.5, LOW, V + R + F - 1)
    a[:, 4] = V + rng.integers(0, R, (N, 2, V)); a[:, 5] = V + R + rng.integers(0, F, (N, 2, V)); a[:, 6] = LOW
    return pack(x, s, q, c, e, a)
def setup_inputs_late(rng):
    x, s, q, c, e, a = parts(rng); g = int(rng.integers(0, 8)); s[:] = 0
    q2, c2 = rng.integers(200, 256, q.shape), rng.integers(200, 256, c.shape); q2[:, g] = q[:, g]; c2[:, g] = c[:, g]
    e[..., V - R:] = np.where(rng.random((N, 8, 1, R)) < 0.5, 2 * V, e[..., V - R:])
    return pack(x, s, q2, c2, e, a)
def setup_inputs_spread(rng):
    x, s, q, c, e, a = parts(rng)
    def u(n):
        return np.minimum((np.exp2(8 * rng.random((N, 8, 1, n))) * rng.random((N, 8, 16, n))).astype(np.int64), 255)
    x = np.where(x > 0, np.minimum(np.exp2(8 * rng.random(x.shape)).astype(np.int64), 255), 0)
    x = rich(rng, x, np.maximum(u(V), 1))
    m = rng.random((N, 8, 16, V)) < rng.random((N, 8, 1, V)) ** 3
    return pack(x, u(R), u(R), u(F), np.where(m, under(rng, (N, 8, 16, V), TOP), 2 * V), a)
def check_inputs(d):
    bad = []
    for k in ("piv", "safe", "lem", "leaf"):
        v = np.asarray(d[k]).astype(np.float32)
        if not np.all((v >= 0) & (v <= 255) & (v == np.floor(v))): bad.append("whole numbers from 0 to 255 in " + k)
    e = np.asarray(d["uses"]).astype(np.int64)
    if not np.all(((e >= 0) & (e < TOP)) | (e == 2 * V)): bad.append("range of uses")
    a = np.stack([gentries(v) for v in d["prem"]]).astype(np.int64).reshape(N, 8, 2, V)
    if not np.all((a >= LOW) & (a < V + R + F)): bad.append("range of prem")
    return bad
def least(S, e):
    return np.stack([[np.min(np.take(S[q, g], e[q, g], axis=1), axis=1) for g in range(8)] for q in range(N)])
def splice(e, st):
    K = np.zeros((N, 8, 1, 2 * V + 1), bool)
    K[:, :, 0, 2 * R:2 * V:2] = st[..., R:] == 1; K[:, :, 0, 2 * R + 1:2 * V:2] = st[..., R:] == 2
    loose = np.take_along_axis(K, e, 3); has = np.any(loose, axis=2, keepdims=True); j = np.argmax(loose, axis=2)[:, :, None]
    this = (np.arange(16)[:, None] == j) & has
    u = np.take_along_axis(e, j, 2) >> 1
    t = np.roll(np.take_along_axis(e, np.where(has, u - R, 0), 3), 8, axis=2)
    hit = np.any((t != 2 * V) & (e != 2 * V) & ~this, axis=2, keepdims=True)
    return np.where(has & ~hit, np.where(t != 2 * V, t, np.where(this, 2 * V, e)), e)
def reference(piv, safe, lem, leaf, uses, prem):
    def w(v):
        return v.astype(np.float32).astype(np.int64).reshape(N, 8, 16, -1)
    x = w(piv); nx = np.roll(x, 8, axis=2)
    s = np.full((N, 8, 16, V), 255, np.int64); s[..., :R] = w(safe)
    C = np.zeros((N, 8, 16, V + R + F), np.int64); C[..., V:V + R] = w(lem); C[..., V + R:] = w(leaf)
    e = uses.astype(np.int64).reshape(N, 8, 16, V)
    a = np.stack([gentries(v) for v in prem]).astype(np.int64).reshape(N, 8, 2, V)
    st = np.zeros((N, 8, V), np.int64); S = np.full((N, 8, 16, 2 * V + 1), 255, np.int64); gs = None
    for rnd in range(RO):
        old = st[:, :, None] > 0
        if rnd:
            s[..., :R] = np.where(old[..., :R], s[..., :R], np.roll(gs, 1, axis=0))
            C[..., V:V + R] = np.roll(C[..., :R], -1, axis=0)
            e = splice(e, st)
        for l in range(L + 1):
            i, j = AT[l], AT[l + 1]
            if l: s[..., i:j] = np.where(old[..., i:j], s[..., i:j], least(S, e[..., i - R:j - R]))
            y, p, n = s[..., i:j], x[..., i:j], nx[..., i:j]; b = st[..., i:j]
            b = np.where(b > 0, b, np.where(np.all(y >= p, axis=2), 1, np.where(np.all(y >= n, axis=2), 2, 0)))
            st[..., i:j] = b; b = b[:, :, None]
            S[..., 2 * i:2 * j:2] = np.where(b == 0, np.maximum(y, p), np.where(b == 1, y, 255))
            S[..., 2 * i + 1:2 * j:2] = np.where(b == 0, np.maximum(y, n), np.where(b == 2, y, 255))
        gs = least(S, e[..., V - R:])
        for l in range(L, -1, -1):
            i, j = AT[l], AT[l + 1]; p, n = x[..., i:j], nx[..., i:j]; b = st[..., i:j]
            A = np.take_along_axis(C, a[:, :, :1, i:j], 3); B = np.take_along_axis(C, a[:, :, 1:, i:j], 3)
            b = np.where(b > 0, b, np.where(~np.all(A >= p, axis=2), 1, np.where(~np.all(B >= n, axis=2), 2, 0)))
            st[..., i:j] = b; b = b[:, :, None]
            C[..., i:j] = np.where(b == 1, A, np.where(b == 2, B, np.maximum(np.where(p > 0, 0, A), np.where(n > 0, 0, B))))
    return {"yc": np.ascontiguousarray(C[..., :V]).reshape(N, 128, V).astype(np.float32).astype(BF), "ys": np.concatenate([s, gs], axis=3).reshape(N, 128, V + R).astype(np.float32).astype(BF)}

@@ -1,0 +1,561 @@
+from concourse.mybir import dt, AluOpType, AxisListType, ActivationFunctionType
+
+EM0 = 1024
+EC0 = 2560
+TW = 5120
+_D = ((128, "d"), (128, "d"))
+_P = ((128, "p"), (128, "d"))
+KNOB = {"gch": 32, "kch": 32, "lat": 0.09, "self": 0.06, "pen": 0.3,
+        "post": {1: ((128, "p"), (64, "p"), (64, "d")), 2: _P, 3: _P}, "post0": {1: _D, 2: _D, 3: _D}}
+
+WID = {"bfloat16": {"tab": TW, "kt": TW, "ct": 1792, "s0": 256, "km": 256, "xn": 2560, "mxn": 2560, "fl": 2560, "f0": 512, "em": 1280,
+                    "ones": 128, "c256": 256, "rs": 2048, "cm": 3328, "wm": 2048, "ab": 1024, "vv": 1024, "ma": 512, "vx": 2048,
+                    "th": 1280, "hh": 1280, "sp": 1280, "gt0": 4096, "gt1": 4096, "sc0": 4096, "sc1": 4096, "sc2": 4096,
+                    "kg2": 4096, "kg3": 4096, "kg4": 4096, "kg5": 4096, "gs1": 256, "gs2": 256, "gs3": 256,
+                    "lg1": 256, "lg2": 256, "lc1": 256, "lc2": 256},
+       "float32": {"e1": 1280, "e2": 1280, "e3": 1280, "off": 1280, "idx": 1024, "cf": 512, "lt": 1280, "dq": 256, "bias": 1, "nb": 2,
+                   "bt": 1280, "tu": 1280},
+       "int32": {"us": 1280, "ey": 1280, "ez": 1280, "pr": 160, "pi": 1, "pj": 1, "oi": 80},
+       "uint16": {"pu": 160, "of1": 1280, "of2": 1280, "of3": 1280, "eu2": 1280, "ou": 80}}
+SCRATCH = {}
+for _t in WID:
+    for _n in WID[_t]:
+        SCRATCH[_n] = ("sbuf", [128, WID[_t][_n]], _t)
+BANKS = ["b%d" % k for k in range(8)]
+for _n in BANKS:
+    SCRATCH[_n] = ("psum", [128, 512], "float32")
+NDMA = 24
+SEMAPHORES = ["sv", "sa", "sp", "sg"] + ["d%d" % i for i in range(NDMA)] + [a + b for a in ("ag", "ac", "og", "oc") for b in "12"]
+
+A = AluOpType
+AF = ActivationFunctionType
+CMN = ["I", "B1", "BLK", "P1", "P2", "PT", "U1", "U2", "U", "Bm256", "Bp256", "Bm8M", "Bm2048", "Bp2048", "Bp64k", "Bm64k", "Bm1",
+       "Ip512", "Im512", "Ipw", "Imw", "Im4096", "PT8k", "Im1", "Ip256", "R"]
+CFN = ["If", "Imf", "PTf", "Bf"]
+
+
+def ap(name, lo, n, step=1):
+    return (name, lo, lo + (n - 1) * step + 1, step)
+
+
+def res(T, a):
+    if a[0] == "ind":
+        return res(T, a[1]).indirect(res(T, a[2]))
+    return T[a[0]][:, a[1]:a[2]] if a[3] == 1 else T[a[0]][:, a[1]:a[2]:a[3]]
+
+
+def cm(n):
+    return ap("cm", 128 * CMN.index(n), 128)
+
+
+def cf(n):
+    return ap("cf", 128 * CFN.index(n), 128)
+
+
+def width(a):
+    return (a[2] - a[1] + a[3] - 1) // a[3]
+
+
+def build():
+    ops, hist = [], {}
+    CY, GC, PC, PO = 1.04e-3, 1.62e-3, 0.5e-3, 0.025
+    two = list(WID["bfloat16"]) + list(WID["uint16"])
+
+    def regs(a):
+        return [a[1], a[2]] if a[0] == "ind" else [a]
+
+    def add(eng, fn, rd, wr, cost, kind="c", **kw):
+        i = len(ops)
+        deps = {}
+        rr = [x for a in rd for x in regs(a)]
+        ww = [x for a in wr for x in regs(a)]
+        for w, xs in ((False, rr), (True, ww)):
+            for nm, lo, hi, st in xs:
+                for (j, l2, h2, s2, w2) in hist.get(nm, []):
+                    if lo < h2 and l2 < hi and (w or w2) and not (st == s2 and (lo - l2) % st):
+                        deps[j] = True
+                    elif nm in BANKS:
+                        deps.setdefault(j, False)
+        for x in ww:
+            if x[0] not in BANKS and x[3] == 1:
+                hist[x[0]] = [e for e in hist.get(x[0], []) if not (x[1] <= e[1] and e[2] <= x[2])]
+        for w, xs in ((False, rr), (True, ww)):
+            for x in xs:
+                hist.setdefault(x[0], []).append((i, x[1], x[2], x[3], w))
+                if x[0] in BANKS:
+                    hist[x[0]] = hist[x[0]][-70:]
+        d = {"i": i, "eng": eng, "fn": fn, "deps": deps, "cost": cost, "kind": kind}
+        d.update(kw)
+        ops.append(d)
+        return i
+
+    def tt(out, i0, i1, op):
+        n = width(i1)
+        c = n * GC if i0[0] == "ind" else n * CY * (1 if i0[0] in BANKS or i1[0] in BANKS else 2)
+        return add("v", lambda q, X: q.tensor_tensor(res(X["T"], out), res(X["T"], i0), res(X["T"], i1), op), [i0, i1], [out], 0.06 + c)
+
+    def half(out, i0):
+        return 0.06 + width(i0) * CY * (0.5 if out[0] in two and i0[0] in two else 1)
+
+    def ts(out, i0, s1, s2, o1, o2=None):
+        def f(q, X):
+            a, b = res(X["T"], out), res(X["T"], i0)
+            return q.tensor_scalar(a, b, s1, None, o1) if o2 is None else q.tensor_scalar(a, b, s1, s2, o1, o2)
+        return add("v", f, [i0], [out], half(out, i0))
+
+    def cp(out, i0):
+        return add("v", lambda q, X: q.tensor_copy(res(X["T"], out), res(X["T"], i0)), [i0], [out], half(out, i0))
+
+    def scan(out, d1, n):
+        d0 = ap("rs", 0, n)
+        return add("v", lambda q, X: q.tensor_tensor_scan(res(X["T"], out), res(X["T"], d0), res(X["T"], d1), 255.0, A.max, A.min),
+                   [d0, d1], [out], 0.06 + n * CY * 0.5)
+
+    def memset(out, v):
+        return add("v", lambda q, X: q.memset(res(X["T"], out), v), [], [out], 0.06 + width(out) * CY * 0.5)
+
+    def act(out, i0, func, bias=0.0, scale=1.0):
+        def f(q, X):
+            b = res(X["T"], bias) if isinstance(bias, tuple) else bias
+            return q.activation(res(X["T"], out), res(X["T"], i0), func, bias=b, scale=scale)
+        return add("a", f, [i0] + [x for x in (bias,) if isinstance(x, tuple)], [out], 0.065 + width(i0) * CY)
+
+    def relu(out, i0, scale=1.0):
+        def f(q, X):
+            if X["e"] == "v":
+                return q.tensor_scalar(res(X["T"], out), res(X["T"], i0), scale, 0.0, A.mult, A.max)
+            return q.activation(res(X["T"], out), res(X["T"], i0), AF.Relu, bias=0.0, scale=scale)
+        return add("va", f, [i0], [out], 0.065 + width(i0) * CY)
+
+    def copier(out, src):
+        def f(q, X):
+            if X["e"] == "v":
+                return q.tensor_copy(res(X["T"], out), res(X["T"], src))
+            return q.activation(res(X["T"], out), res(X["T"], src), AF.Copy, bias=0.0, scale=1.0)
+        return f
+
+    def move(out, i0):
+        return add("va", copier(out, i0), [i0], [out], 0.065 + width(i0) * CY)
+
+    def gather(out, win, off, eng="va"):
+        src = ("ind", win, off)
+        return add(eng, copier(out, src), [src], [out], 0.06 + width(off) * 16 * GC, flex=True)
+
+    def mm(out, lt, rhs, st, sp_):
+        c = PO + max(64, width(rhs)) * PC * (4 if lt[0] in ("cf", "bt", "lt") else 1)
+        return add("p", lambda q, X: q.matmul(res(X["T"], out), res(X["T"], lt), res(X["T"], rhs), st, sp_), [lt, rhs], [out], c)
+
+    def group(out, terms):
+        for k, (lt, rhs) in enumerate(terms):
+            mm(out, lt, rhs, k == 0, k == len(terms) - 1)
+
+    def asel(out, i0, pat, op, fill, base, chm):
+        return add("g", lambda q, X: q.affine_select(res(X["T"], out), res(X["T"], i0), pat, op, fill, base, chm),
+                   [i0], [out], 0.2 + width(out) * CY * 2)
+
+    def gmove(out, i0):
+        return asel(out, i0, [[0, width(i0)]], A.is_gt, 0.0, 1, 0)
+
+    def iota(out, pat, base, chm):
+        def f(q, X):
+            if out[0] == "pi":
+                return q.iota(res(X["T"], out), pat, base, chm)
+            return q.iota(res(X["T"], out), pat, base, chm, allow_small_or_imprecise_dtypes=True)
+        return add("g", f, [], [out], 0.16 + width(out) * CY * 2)
+
+    nd = [0]
+
+    def dma(eng, out, i0):
+        nd[0] += 1
+        return add(eng, lambda q, X: q.dma_start(res(X["T"], out), res(X["T"], i0)), [i0], [out], 0.08, "dma", sem="d%d" % nd[0], lat=2.2)
+
+    def send(dst_off, out, i0, arr, loc):
+        def f(q, X):
+            topo, T, core = X["topo"], X["T"], X["core"]
+            dst = T.cores[(X["rank"] + dst_off) % len(T.cores)]
+            rid, pid = topo.addr(dst, core)
+            q.remote_dma(res(T, out), res(T, i0), T.sem[arr], T.sem[loc], pid, rid, topo.mask(core, dst))
+        k = add("g", f, [i0], [], 0.4, "send", sem=loc, lat=3.0, dst=dst_off)
+        add("none", None, [], [out], 0.0, "arr", sem=arr, lat=4.0, after=k, dst=-dst_off)
+
+    dma("a", ap("us", 0, 256), ap("uses", 0, 256))
+    dma("sy", ap("xn", 0, 256), ap("piv", 0, 256))
+    dma("sy", ap("s0", 0, 256), ap("safe", 0, 256))
+    ones = ap("ones", 0, 128)
+    memset(ones, 1.0)
+    asel(cm("I"), ones, [[-1, 128]], A.is_equal, 0.0, 0, 1)
+    asel(cm("B1"), ones, [[-16, 8], [0, 16]], A.is_ge, 0.0, 0, 1)
+    asel(cm("BLK"), cm("B1"), [[16, 8], [0, 16]], A.is_ge, 0.0, 15, -1)
+    asel(cm("P1"), ones, [[-1, 128]], A.is_equal, 0.0, -8, 1)
+    asel(cm("P2"), cm("P1"), [[-1, 128]], A.not_equal, 1.0, 8, 1)
+    tt(cm("PT"), cm("P2"), cm("BLK"), A.mult)
+    memset(ap("rs", 0, 2048), 0.0)
+    memset(ap("rs", 0, 128, 16), 255.0)
+    memset(ap("tab", 0, EC0), 255.0)
+    memset(ap("c256", 0, 256), 256.0)
+    memset(ap("nb", 0, 1), -1024.0)
+    memset(ap("nb", 1, 1), -1.0)
+    for nm, base, sc in (("Im1", "I", -1.0), ("Bm256", "BLK", -256.0), ("Bp256", "BLK", 256.0), ("Bm8M", "BLK", -8388608.0),
+                         ("Ip256", "I", 256.0), ("Bm2048", "BLK", -2048.0),
+                         ("Bp2048", "BLK", 2048.0), ("Bp64k", "BLK", 65536.0), ("Bm64k", "BLK", -65536.0), ("Ip512", "I", 512.0),
+                         ("Ipw", "I", 4194304.0), ("Imw", "I", -4194304.0), ("U1", "BLK", -0.5), ("Bm1", "BLK", -1.0), ("Im512", "I", -512.0),
+                         ("Im4096", "I", -4096.0), ("PT8k", "PT", 8192.0)):
+        act(cm(nm), cm(base), AF.Copy, scale=sc)
+    for nm, base, sc in (("If", "I", 1.0), ("Imf", "I", -1.0), ("PTf", "PT", 1.0), ("Bf", "BLK", 1.0)):
+        act(cf(nm), cm(base), AF.Copy, scale=sc)
+    dma("sy", ap("us", 256, 1024), ap("uses", 256, 1024))
+    for l in range(1, 5):
+        dma("sy", ap("xn", 512 * l, 256), ap("piv", 256 * l, 256))
+    dma("sy", ap("pr", 0, 160), ap("prem", 0, 160))
+    dma("sy", ap("ct", 1280, 256), ap("lem", 0, 256))
+    dma("sy", ap("ct", 1536, 256), ap("leaf", 0, 256))
+
+    def cl(l):
+        return float(1024 - 256 * (l - 1)) if l < 5 else 0.0
+
+    def win(t, l):
+        return ap(t, 256 * (l - 1), EC0 + 512 * l - 256 * (l - 1)) if l < 5 else ap(t, EM0, TW - EM0)
+
+    for l in range(0, 5):
+        b = ap("b%d" % (4 + l % 3), 0, 256)
+        mm(b, cm("PT"), ap("xn", 512 * l, 256), True, True)
+        act(ap("xn", 512 * l + 256, 256), b, AF.Copy)
+        for q in ((1,), (2, 3, 4, 5), (), (), ())[l]:
+            o = 256 * (q - 1)
+            ts(ap("ey", o, 256), ap("us", o, 256), 1536, None, A.add)
+            ts(ap("ez", o, 256), ap("ey", o, 256), 4095, None, A.bitwise_and)
+            ts(ap("of1", o, 256), ap("ez", o, 256), cl(q), None, A.add)
+    iota(ap("ct", 0, 1280), [[0, 1280]], 0, 0)
+    iota(ap("kt", 0, EC0 + 512), [[0, EC0 + 512]], -1, 0)
+    iota(ap("idx", 0, 1024), [[1, 1024]], 7168, 0)
+    iota(ap("pi", 0, 1), [[0, 1]], 0, 1)
+    asel(cm("U2"), cm("U1"), [[1, 128]], A.is_gt, 0.0, 0, -1)
+    asel(cm("U"), cm("U2"), [[-1, 128]], A.not_equal, 0.5, 0, 1)
+    for i in range(16):
+        asel(ap("wm", 128 * i, 128), cm("U"), [[-16, 8], [0, 16]], A.is_equal, 0.0, -i, 1)
+    asel(cm("R"), ones, [[0, 8], [1, 16]], A.is_equal, 0.0, 0, -1)
+    for h in (0, 1):
+        mm(ap("b5", 128 * h, 128), cm("R"), cm("R"), True, True)
+    cp(ap("dq", 0, 256), ap("b5", 0, 256))
+    cp(ap("pu", 0, 160), ap("pr", 0, 160))
+    ts(ap("pj", 0, 1), ap("pi", 0, 1), 15, None, A.bitwise_and)
+    ts(ap("bias", 0, 1), ap("pj", 0, 1), -0.5, 0.5, A.mult, A.add)
+    for l in range(5):
+        ts(ap("mxn", 512 * l, 512), ap("xn", 512 * l, 512), 0.0, None, A.is_equal)
+    for q in range(1, 6):
+        cp(ap("e1", 256 * (q - 1), 256), ap("ez", 256 * (q - 1), 256))
+        if q > 1:
+            act(ap("em", 256 * (q - 1), 256), ap("e1", 256 * (q - 1), 256), AF.Relu, bias=1.0, scale=-1.0)
+
+    def sa(l, k, n=256, c0=0):
+        return ap("f0", k * 256 + c0, n) if l == 0 else ap("kt", EC0 + 512 * l + k + 2 * c0, n, 2)
+
+    cnt = [0]
+
+    def post(r, l, c0, n, how):
+        k = cnt[0] % 2
+        cnt[0] += 1
+        XS, YZ, SS = "b%d" % k, "b%d" % (2 if how == "p" else 2 + k), "b3"
+        s = ap("s0", c0, n) if l == 0 else ap("sc%d" % (l % 3), 16 * c0 + 15, n, 16)
+        for h, a, b in ((0, "Im512", "Ip512"), (1, "Ip512", "Im512")):
+            t = [(cm("I"), ap("xn", 512 * l + 256 * h + c0, n))]
+            if r > 1:
+                t += [(cm(a), sa(l, 0, n, c0)), (cm(b), sa(l, 1, n, c0))]
+            group(ap(XS, h * n, n), t + ([(cm("Im1"), s)] if how == "p" else []))
+        v = 1024 * k
+        da, db = ap("vx", v, n), ap("vx", v + n, n)
+        f = 512 * l + 2 * c0
+        t = EC0 + 512 * l + 2 * c0
+        Y, Z = ap(YZ, 0, n), ap(YZ, n, n)
+        if how == "d":
+            xa, xb = ap(XS, 0, n), ap(XS, n, n)
+            ma, mb = ap("vx", v + 512, n), ap("vx", v + 512 + n, n)
+            tt(da, s, xa, A.is_lt)
+            tt(db, s, xb, A.is_lt)
+        else:
+            relu(ap("vx", v, 2 * n), ap(XS, 0, 2 * n))
+        group(Y, [(cm("I"), ap("c256", 0, n)), (cm("Bm256"), da)])
+        group(Z, [(cm("Bp256"), da), (cm("Bm8M"), db)])
+        if how == "d":
+            tt(ma, s, xa, A.max)
+            tt(mb, s, xb, A.max)
+            tt(ap("tab", t, n, 2), ma, Z, A.max)
+            tt(ap("tab", t + 1, n, 2), mb, Y, A.max)
+        relu(ap("fl", f, 2 * n), ap(YZ, 0, 2 * n), 1.0 / 256)
+        if how == "p":
+            group(ap(SS, 0, n, 2), [(cm("I"), s), (cm("I"), da), (cm("Ip256"), ap("fl", f + n, n))])
+            group(ap(SS, 1, n, 2), [(cm("I"), s), (cm("I"), db), (cm("Ip256"), ap("fl", f, n))])
+            move(ap("tab", t, 2 * n), ap(SS, 0, 2 * n))
+
+    def chunks(n, c):
+        return [(k, min(c, n - k)) for k in range(0, n, c)]
+
+    def splice(r, q):
+        o = 256 * (q - 1)
+        ein, eout = ("e1", "e2") if r == 2 else ("e2", "e3")
+        ku = "of1" if r == 2 else "eu2"
+        kg = "kg%d" % q
+        for k, n in chunks(256, KNOB["kch"]):
+            gather(ap(kg, 16 * k, 16 * n), win("kt", q), ap(ku, o + k, n))
+        group(ap("b4", 0, 256), [(ap("wm", 128 * i, 128), ap(kg, i, 256, 16)) for i in range(16)])
+        th, bt, e = ap("th", o, 256), ap("bt", o, 256), ap(ein, o, 256)
+        act(th, ap("b4", 0, 256), AF.Relu, bias=ap("bias", 0, 1))
+        tt(bt, th, e, A.mult)
+        for h in (0, 1):
+            mm(ap("b4", 256 + 128 * h, 128), ap("bt", o + 128 * h, 128), cf("Bf"), True, True)
+        tt(ap("lt", o, 256), ap("dq", 0, 256), ap("b4", 256, 256), A.mult)
+        for h in (0, 1):
+            mm(ap("b4", 8 * h, 8), ap("lt", o + 128 * h, 128), ap("cf", 128 * CFN.index("Bf"), 8, 16), True, True)
+        oi, ou = ap("oi", 16 * (q - 1), 16), ap("ou", 16 * (q - 1), 16)
+        ts(oi, ap("b4", 0, 16), 0.5, -1024.25, A.mult, A.add)
+        cp(ou, oi)
+        tu = ap("tu", o, 256)
+        gather(tu, ap(ein, 0, 1024), ou)
+        group(ap("b5", 0, 256), [(cm("PT8k"), th), (cm("PT8k"), ap("em", o, 256))])
+        group(ap("b6", 0, 256), [(cf("PTf"), tu), (cf("Imf"), bt)])
+        hh, sp_ = ap("hh", o, 256), ap("sp", o, 256)
+        tt(hh, tu, ap("b5", 0, 256), A.is_gt)
+        group(ap("b5", 256, 256), [(cm("BLK"), th), (cm("Bm1"), hh)])
+        relu(sp_, ap("b5", 256, 256))
+        tt(ap("b6", 256, 256), sp_, ap("b6", 0, 256), A.mult)
+        tt(ap(eout, o, 256), e, ap("b6", 256, 256), A.add)
+        if r == 2:
+            act(ap("em", o, 256), ap(eout, o, 256), AF.Relu, bias=1.0, scale=-1.0)
+        offs(r, q, eout)
+
+    def offs(r, q, src):
+        o = 256 * (q - 1)
+        of = ap("of%d" % r, o, 256)
+        if q == 5:
+            cp(of, ap(src, o, 256))
+            if r == 2:
+                cp(ap("eu2", o, 256), of)
+            return
+        P = ap("b7", 256 * (q % 2), 256)
+        group(P, [(cf("If"), ap(src, o, 256)), (cm("Im4096"), sa(q, 0)), (cm("Im4096"), sa(q, 1))])
+        tt(ap("off", o, 256), ap("idx", o, 256), P, A.max)
+        ts(of, ap("off", o, 256), cl(q) - 8192.0, None, A.add)
+        if r == 2 and q > 1:
+            ts(ap("eu2", o, 256), ap(src, o, 256), cl(q), None, A.add)
+
+    def sets(r, l):
+        o = 256 * (l - 1)
+        c0 = 0
+        gt, sc = "gt%d" % (l % 2), "sc%d" % (l % 3)
+        for p, how in (KNOB["post"][r] if l < 5 else _D):
+            for k, n in chunks(p, KNOB["gch"]):
+                gather(ap(gt, 16 * (c0 + k), 16 * n), win("tab", l), ap("of%d" % r, o + c0 + k, n))
+            scan(ap(sc, 16 * c0, 16 * p), ap(gt, 16 * c0, 16 * p), 16 * p)
+            if l < 5:
+                post(r, l, c0, p, how)
+            c0 += p
+        gmove(ap("tab", o, 256) if l < 5 else ap("gs%d" % r, 0, 256), ap(sc, 15, 256, 16))
+
+    def up(r, l):
+        X, PA, PB = "b%d" % (l % 2), ap("b%d" % (2 + l % 2), 0, 256), ap("b%d" % (4 + l % 2), 0, 256)
+        h = l % 2
+        mm(ap(X, 0, 256), cm("I"), ap("xn", 512 * l, 256), True, True)
+        for P, k, a, b in ((PA, 0, "Ipw", "Imw"), (PB, 256, "Imw", "Ipw")):
+            mm(P, cm("Ip512"), ap("mxn", 512 * l + k, 256), True, False)
+            c0 = 0
+            for n, how in KNOB["post" if l else "post0"][r]:
+                f = 512 * l + 2 * c0
+                mm(ap(P[0], c0, n), cm(a), ap("fl", f, n), False, False)
+                mm(ap(P[0], c0, n), cm(b), ap("fl", f + n, n), False, False)
+                c0 += n
+        w = ap("ct", 0, 1792)
+        av, bv = ap("ab", 512 * h, 256), ap("ab", 512 * h + 256, 256)
+        va, vb = ap("vv", 512 * h, 256), ap("vv", 512 * h + 256, 256)
+        ua, ub = ap("pu", 16 * l, 16), ap("pu", 80 + 16 * l, 16)
+        gather(av, w, ua, "a")
+        tt(vb, ("ind", w, ub), ap("xn", 512 * l + 256, 256), A.is_lt)
+        gather(bv, w, ub, "a")
+        mm(PA, cm("Bm2048"), vb, False, False)
+        mm(PB, cm("Bp2048"), vb, False, False)
+        tt(va, av, ap(X, 0, 256), A.is_lt)
+        mm(PA, cm("Bp64k"), va, False, True)
+        mm(PB, cm("Bm64k"), va, False, True)
+        ma, mb = ap("ma", 256 * h, 256), ap(X, 256, 256)
+        tt(ma, av, PA, A.min)
+        tt(mb, bv, PB, A.min)
+        tt(ap("ct", 256 * l, 256), ma, mb, A.max)
+        if r < 3:
+            for k, P in ((0, PA), (1, PB)):
+                if l:
+                    act(sa(l, k), P, AF.Sign, bias=ap("nb", 0, 1))
+                else:
+                    act(sa(0, k), P, AF.Relu, bias=ap("nb", 1, 1), scale=1.0 / 1024)
+
+    for r in (1, 2, 3):
+        if r > 1:
+            group(ap("b6", 0, 256), [(cm("Ip512"), sa(0, 0)), (cm("Ip512"), sa(0, 1))])
+            group(ap("b3", 0, 256), [(cm("I"), ap("lg%d" % (r - 1), 0, 256)), (cm("Im512"), sa(0, 0)), (cm("Im512"), sa(0, 1))])
+            tt(ap("km", 0, 256), ap("s0", 0, 256), ap("b6", 0, 256), A.min)
+            tt(ap("s0", 0, 256), ap("km", 0, 256), ap("b3", 0, 256), A.max)
+        c0 = 0
+        for n, how in KNOB["post0"][r]:
+            post(r, 0, c0, n, how)
+            c0 += n
+        if r > 1:
+            offs(r, 1, "e1")
+            if r == 2:
+                gmove(ap("e2", 0, 256), ap("e1", 0, 256))
+            for q in (2, 3, 4, 5):
+                splice(r, q)
+        for l in (1, 2, 3, 4):
+            sets(r, l)
+        if r > 1:
+            gmove(ap("ct", 1280, 256), ap("lc%d" % (r - 1), 0, 256))
+        sets(r, 5)
+        if r < 3:
+            send(1, ap("lg%d" % r, 0, 256), ap("gs%d" % r, 0, 256), "ag%d" % r, "og%d" % r)
+        else:
+            dma("sy", ap("ys", 0, 256), ap("s0", 0, 256))
+            dma("sy", ap("ys", 256, 1024), ap("tab", 0, 1024))
+            dma("sy", ap("ys", 1280, 256), ap("gs3", 0, 256))
+        for l in (4, 3, 2, 1, 0):
+            up(r, l)
+            if r == 3 and l == 1:
+                dma("sy", ap("yc", 256, 1024), ap("ct", 256, 1024))
+        if r < 3:
+            send(-1, ap("lc%d" % r, 0, 256), ap("ct", 0, 256), "ac%d" % r, "oc%d" % r)
+        else:
+            dma("sy", ap("yc", 0, 256), ap("ct", 0, 256))
+    return ops
+
+
+def order(ops):
+    n = len(ops)
+    succ = [[] for _ in range(n)]
+    for o in ops:
+        for j in o["deps"]:
+            succ[j].append(o["i"])
+        if o["kind"] == "arr":
+            succ[o["after"]].append(o["i"])
+    prio = [0.0] * n
+    for i in range(n - 1, -1, -1):
+        t = max([prio[j] for j in succ[i]] + [0.0])
+        prio[i] = t + ops[i]["cost"] + ops[i].get("lat", 0.0) + KNOB["lat"]
+    npred = [len(o["deps"]) + (1 if o["kind"] == "arr" else 0) for o in ops]
+    fin, place = [0.0] * n, [None] * n
+    ready, free = [], {"v": 0.0, "a": 0.0, "p": 0.0, "g": 0.0, "sy": 0.0}
+    queues = {e: [] for e in free}
+
+    def when(i, e):
+        t = 0.0
+        for j, raw in ops[i]["deps"].items():
+            if place[j] == e and ops[j]["kind"] == "c":
+                t = max(t, fin[j] + (KNOB["self"] if raw and e != "p" else 0.0))
+            else:
+                t = max(t, fin[j] + KNOB["lat"])
+        return t
+
+    def done(i, t, e):
+        fin[i], place[i] = t, e
+        for j in succ[i]:
+            npred[j] -= 1
+            if npred[j] == 0:
+                if ops[j]["kind"] == "arr":
+                    done(j, max(fin[ops[j]["after"]] + 1.0, when(j, "none")), "none")
+                else:
+                    ready.append(j)
+    for i in range(n):
+        if npred[i] == 0 and ops[i]["kind"] != "arr":
+            ready.append(i)
+    starts = [0.0] * n
+    while ready:
+        best = None
+        for e in free:
+            for i in ready:
+                g = ops[i]["eng"]
+                if e != g and not (g == "va" and e in "va"):
+                    continue
+                t = max(free[e], when(i, e))
+                key = (t + (KNOB["pen"] if g == "va" and e == "v" and "flex" in ops[i] else 0.0), -prio[i], i)
+                if best is None or key < best[0]:
+                    best = (key, i, e, t)
+        _, i, e, t = best
+        ready.remove(i)
+        free[e] = t + ops[i]["cost"]
+        starts[i] = t
+        queues[e].append(i)
+        done(i, t + ops[i]["cost"] + ops[i].get("lat", 0.0), e)
+    return queues, place, starts, max(fin)
+
+
+CACHE = {}
+
+
+def plan():
+    if "p" not in CACHE:
+        ops = build()
+        q, place, starts, end = order(ops)
+        CACHE["p"] = (ops, q, place, starts, end)
+    return CACHE["p"]
+
+
+SEM = {"v": "sv", "a": "sa", "p": "sp", "g": "sg"}
+
+
+def rank_program(g, core, T, topo):
+    rank = T.rank_of(core)
+    if rank is None:
+        return
+    ops, queues, place, starts, end = plan()
+    Q = {"v": g.vector, "a": g.scalar, "p": g.tensor, "g": g, "sy": g.sync}
+    number = {}
+    for e in queues:
+        k = 0
+        for i in queues[e]:
+            if ops[i]["kind"] == "c":
+                k += 1
+                number[i] = (SEM[e], k)
+    total = {}
+    for i, o in enumerate(ops):
+        if o["kind"] == "dma":
+            number[i] = (o["sem"], 16)
+        elif o["kind"] != "c":
+            other = T.cores[(rank + o["dst"]) % len(T.cores)]
+            number[i] = (o["sem"], len(topo.engines(core, other) if o["kind"] == "send" else topo.engines(other, core)))
+        s, k = number[i]
+        total[s] = max(total.get(s, 0), k)
+    known = {e: {} for e in queues}
+    after = {}
+
+    def learn(a, b):
+        for s, k in b.items():
+            if a.get(s, 0) < k:
+                a[s] = k
+    emitted = {}
+    pending = {e: list(queues[e]) for e in queues}
+    while any(pending.values()):
+        for e in pending:
+            while pending[e]:
+                i = pending[e][0]
+                o = ops[i]
+                if any(j not in emitted and ops[j]["kind"] != "arr" for j in o["deps"]):
+                    break
+                need = {}
+                for j, raw in o["deps"].items():
+                    if place[j] == e and ops[j]["kind"] == "c" and (e == "p" or not raw):
+                        continue
+                    s, k = number[j]
+                    need[s] = max(need.get(s, 0), k)
+                kn = known[e]
+                todo = [(s, k) for s, k in need.items() if kn.get(s, 0) < k]
+                for s, k in todo:
+                    if any((s2, k2) != (s, k) and after.get((s2, k2), {}).get(s, 0) >= k for s2, k2 in todo):
+                        continue
+                    Q[e].wait_ge(T.sem[s], k)
+                    learn(kn, {s: k})
+                    learn(kn, after.get((s, k), {}))
+                ins = o["fn"](Q[e], {"T": T, "topo": topo, "core": core, "rank": rank, "e": e})
+                s, k = number[i]
+                if o["kind"] != "send":
+                    ins.then_inc(T.sem[s], 1 if o["kind"] == "c" else 16)
+                after[(s, k)] = dict(kn)
+                emitted[i] = True
+                pending[e].pop(0)
+    for s in sorted(total):
+        if known["g"].get(s, 0) < total[s]:
+            g.wait_ge(T.sem[s], total[s])

@@ -1,26 +1,32 @@
 from concourse.mybir import dt, AluOpType, AxisListType, ActivationFunctionType
 
-EM0 = 1024
-EC0 = 2560
-TW = 5120
-_D = ((128, "d"), (128, "d"))
-_P = ((128, "p"), (128, "d"))
+EC = 16
+OWN = EC + 2560
+TW = OWN + 1024
+MID = 1800
+NEG = -8192.0
+UC = 128
+_H = ((128, "h"), (128, "n"))
+_N = ((128, "h"), (128, "n"))
 KNOB = {"gch": 32, "kch": 32, "lat": 0.09, "self": 0.06, "pen": 0.3,
-        "post": {1: ((128, "p"), (64, "p"), (64, "d")), 2: _P, 3: _P}, "post0": {1: _D, 2: _D, 3: _D}}
+        "lay": {1: {1: _N, 2: _H, 3: _H, 4: _H, 5: _H}, 2: {1: _H, 2: _H, 3: _H, 4: _H, 5: _H}, 3: {1: _H, 2: _H, 3: _H, 4: _H, 5: _H}},
+        "root": (128, 128), "up": {1: "L", 2: "L", 3: "L"}}
 
-WID = {"bfloat16": {"tab": TW, "kt": TW, "ct": 1792, "s0": 256, "km": 256, "xn": 2560, "mxn": 2560, "fl": 2560, "f0": 512, "em": 1280,
-                    "ones": 128, "c256": 256, "rs": 2048, "cm": 3328, "wm": 2048, "ab": 1024, "vv": 1024, "ma": 512, "vx": 2048,
-                    "th": 1280, "hh": 1280, "sp": 1280, "gt0": 4096, "gt1": 4096, "sc0": 4096, "sc1": 4096, "sc2": 4096,
-                    "kg2": 4096, "kg3": 4096, "kg4": 4096, "kg5": 4096, "gs1": 256, "gs2": 256, "gs3": 256,
+WID = {"bfloat16": {"tab": TW, "kt0": TW, "kt1": TW, "k0": 512, "ct": 3072, "s0": 256, "km": 256, "mk": 1280,
+                    "ones": 128, "c8k": 256, "cy": 512, "r16": 2048, "r8": 2048, "r2": 512, "cm": 128 * 28, "wm": 2048,
+                    "mx": 1024, "ab": 1024, "uu": 1024, "hh": 1280, "ga0": 4096, "ga1": 4096, "gb0": 2048, "gb1": 2048,
+                    "sc0": 4096, "sc1": 4096, "sc2": 4096, "kg2": 4096, "kg3": 4096, "kg4": 4096, "kg5": 4096,
+                    "gs1": 256, "gs2": 256, "gs3": 256, "rc1": 256, "rc2": 256, "ycb": 1280,
                     "lg1": 256, "lg2": 256, "lc1": 256, "lc2": 256},
-       "float32": {"e1": 1280, "e2": 1280, "e3": 1280, "off": 1280, "idx": 1024, "cf": 512, "lt": 1280, "dq": 256, "bias": 1, "nb": 2,
-                   "bt": 1280, "tu": 1280},
-       "int32": {"us": 1280, "ey": 1280, "ez": 1280, "pr": 160, "pi": 1, "pj": 1, "oi": 80},
-       "uint16": {"pu": 160, "of1": 1280, "of2": 1280, "of3": 1280, "eu2": 1280, "ou": 80}}
+       "float16": {"v1": 1280, "e1": 1280, "e2": 1280, "e3": 1280, "em": 1280, "tu": 1280, "t1": 1280, "eo": 1280, "idx": 1024},
+       "float32": {"et2": 1032, "et3": 1032, "lt": 1280, "dq": 256, "bf8": 8, "nb": 2, "idf": 1024, "p1": 160, "p2": 160, "p3": 160},
+       "int32": {"us": 1280, "pr": 160, "oi": 80},
+       "uint16": {"pu": 160, "of1": 1280, "of2": 1280, "of3": 1280, "ou": 80}}
 SCRATCH = {}
 for _t in WID:
     for _n in WID[_t]:
         SCRATCH[_n] = ("sbuf", [128, WID[_t][_n]], _t)
+SCRATCH["xn"] = ("sbuf", [128, 1280 // UC, 2 * UC], "bfloat16")
 BANKS = ["b%d" % k for k in range(8)]
 for _n in BANKS:
     SCRATCH[_n] = ("psum", [128, 512], "float32")
@@ -29,9 +35,12 @@ SEMAPHORES = ["sv", "sa", "sp", "sg"] + ["d%d" % i for i in range(NDMA)] + [a + 
 
 A = AluOpType
 AF = ActivationFunctionType
-CMN = ["I", "B1", "BLK", "P1", "P2", "PT", "U1", "U2", "U", "Bm256", "Bp256", "Bm8M", "Bm2048", "Bp2048", "Bp64k", "Bm64k", "Bm1",
-       "Ip512", "Im512", "Ipw", "Imw", "Im4096", "PT8k", "Im1", "Ip256", "R"]
-CFN = ["If", "Imf", "PTf", "Bf"]
+SCALED = (("Bm51", "BLK", -2.0 ** 51), ("Bp51", "BLK", 2.0 ** 51), ("Bp65", "BLK", 2.0 ** 65), ("Bm65", "BLK", -2.0 ** 65),
+          ("Im1", "I", -1.0), ("Im16k", "I", -16384.0), ("I1520", "I", 1520.0), ("U1", "BLK", 16384.0),
+          ("Ipw", "I", 2.0 ** -11), ("Imw", "I", -2.0 ** -11), ("I512", "I", 512.0), ("PT512", "PT", 512.0),
+          ("Bp25", "BLK", 2.0 ** 25), ("Bm25", "BLK", -2.0 ** 25), ("Bp12", "BLK", 4096.0), ("Bm12", "BLK", -4096.0),
+          ("Bpx", "BLK", 2.0 ** -7), ("Bmx", "BLK", -2.0 ** -7), ("Bm1", "BLK", -1.0), ("Im4", "I", -4.0))
+CMN = ["I", "BLK", "P0", "P1", "PT", "D0", "D1", "B1"] + [x[0] for x in SCALED]
 
 
 def ap(name, lo, n, step=1):
@@ -41,6 +50,9 @@ def ap(name, lo, n, step=1):
 def res(T, a):
     if a[0] == "ind":
         return res(T, a[1]).indirect(res(T, a[2]))
+    if a[0] == "xn":
+        u = a[1] // (2 * UC)
+        return T["xn"][:, u, a[1] - 2 * UC * u:a[2] - 2 * UC * u]
     return T[a[0]][:, a[1]:a[2]] if a[3] == 1 else T[a[0]][:, a[1]:a[2]:a[3]]
 
 
@@ -48,23 +60,23 @@ def cm(n):
     return ap("cm", 128 * CMN.index(n), 128)
 
 
-def cf(n):
-    return ap("cf", 128 * CFN.index(n), 128)
-
-
 def width(a):
     return (a[2] - a[1] + a[3] - 1) // a[3]
+
+
+def cost(o, e):
+    return o["cost"][e] if isinstance(o["cost"], dict) else o["cost"]
 
 
 def build():
     ops, hist = [], {}
     CY, GC, PC, PO = 1.04e-3, 1.62e-3, 0.5e-3, 0.025
-    two = list(WID["bfloat16"]) + list(WID["uint16"])
+    two = list(WID["bfloat16"]) + list(WID["uint16"]) + list(WID["float16"]) + ["xn"]
 
     def regs(a):
         return [a[1], a[2]] if a[0] == "ind" else [a]
 
-    def add(eng, fn, rd, wr, cost, kind="c", **kw):
+    def add(eng, fn, rd, wr, c, kind="c", **kw):
         i = len(ops)
         deps = {}
         rr = [x for a in rd for x in regs(a)]
@@ -84,7 +96,7 @@ def build():
                 hist.setdefault(x[0], []).append((i, x[1], x[2], x[3], w))
                 if x[0] in BANKS:
                     hist[x[0]] = hist[x[0]][-70:]
-        d = {"i": i, "eng": eng, "fn": fn, "deps": deps, "cost": cost, "kind": kind}
+        d = {"i": i, "eng": eng, "fn": fn, "deps": deps, "cost": c, "kind": kind}
         d.update(kw)
         ops.append(d)
         return i
@@ -106,48 +118,44 @@ def build():
     def cp(out, i0):
         return add("v", lambda q, X: q.tensor_copy(res(X["T"], out), res(X["T"], i0)), [i0], [out], half(out, i0))
 
-    def scan(out, d1, n):
-        d0 = ap("rs", 0, n)
-        return add("v", lambda q, X: q.tensor_tensor_scan(res(X["T"], out), res(X["T"], d0), res(X["T"], d1), 255.0, A.max, A.min),
-                   [d0, d1], [out], 0.06 + n * CY * 0.5)
+    def scan(out, d0, d1, first, o0, o1):
+        return add("v", lambda q, X: q.tensor_tensor_scan(res(X["T"], out), res(X["T"], d0), res(X["T"], d1), first, o0, o1),
+                   [d0, d1], [out], half(out, d1))
 
     def memset(out, v):
-        return add("v", lambda q, X: q.memset(res(X["T"], out), v), [], [out], 0.06 + width(out) * CY * 0.5)
+        return add("v", lambda q, X: q.memset(res(X["T"], out), v), [], [out], 0.06 + width(out) * CY * (0.5 if out[0] in two else 1))
 
-    def act(out, i0, func, bias=0.0, scale=1.0):
+    def either(out, i0, s1, s2, o1, o2, func, scale, bias):
         def f(q, X):
-            b = res(X["T"], bias) if isinstance(bias, tuple) else bias
-            return q.activation(res(X["T"], out), res(X["T"], i0), func, bias=b, scale=scale)
-        return add("a", f, [i0] + [x for x in (bias,) if isinstance(x, tuple)], [out], 0.065 + width(i0) * CY)
-
-    def relu(out, i0, scale=1.0):
-        def f(q, X):
+            a, b = res(X["T"], out), res(X["T"], i0)
             if X["e"] == "v":
-                return q.tensor_scalar(res(X["T"], out), res(X["T"], i0), scale, 0.0, A.mult, A.max)
-            return q.activation(res(X["T"], out), res(X["T"], i0), AF.Relu, bias=0.0, scale=scale)
-        return add("va", f, [i0], [out], 0.065 + width(i0) * CY)
+                if o1 is None:
+                    return q.tensor_copy(a, b)
+                return q.tensor_scalar(a, b, s1, None, o1) if o2 is None else q.tensor_scalar(a, b, s1, s2, o1, o2)
+            return q.activation(a, b, func, bias=res(X["T"], bias) if isinstance(bias, tuple) else bias, scale=scale)
+        rd = [i0] + [x for x in (bias,) if isinstance(x, tuple)]
+        if i0[0] == "ind":
+            return add("va", f, rd, [out], 0.06 + width(out) * GC, flex=True)
+        return add("va", f, rd, [out], {"v": half(out, i0), "a": 0.065 + width(i0) * CY})
 
-    def copier(out, src):
-        def f(q, X):
-            if X["e"] == "v":
-                return q.tensor_copy(res(X["T"], out), res(X["T"], src))
-            return q.activation(res(X["T"], out), res(X["T"], src), AF.Copy, bias=0.0, scale=1.0)
-        return f
+    def scale(out, i0, c):
+        return either(out, i0, c, None, A.mult, None, AF.Copy, c, 0.0)
 
-    def move(out, i0):
-        return add("va", copier(out, i0), [i0], [out], 0.065 + width(i0) * CY)
+    def relu(out, i0, c=1.0):
+        return either(out, i0, c, 0.0, A.mult, A.max, AF.Relu, c, 0.0)
 
     def gather(out, win, off, eng="va"):
-        src = ("ind", win, off)
-        return add(eng, copier(out, src), [src], [out], 0.06 + width(off) * 16 * GC, flex=True)
+        k = either(out, ("ind", win, off), None, None, None, None, AF.Copy, 1.0, 0.0)
+        ops[k]["eng"] = eng
+        return k
 
     def mm(out, lt, rhs, st, sp_):
-        c = PO + max(64, width(rhs)) * PC * (4 if lt[0] in ("cf", "bt", "lt") else 1)
+        c = PO + max(64, width(rhs)) * PC * (4 if lt[0] == "lt" else 1)
         return add("p", lambda q, X: q.matmul(res(X["T"], out), res(X["T"], lt), res(X["T"], rhs), st, sp_), [lt, rhs], [out], c)
 
     def group(out, terms):
-        for k, (lt, rhs) in enumerate(terms):
-            mm(out, lt, rhs, k == 0, k == len(terms) - 1)
+        for k, t in enumerate(terms):
+            mm(t[2] if len(t) > 2 else out, cm(t[0]) if isinstance(t[0], str) else t[0], t[1], k == 0, k == len(terms) - 1)
 
     def asel(out, i0, pat, op, fill, base, chm):
         return add("g", lambda q, X: q.affine_select(res(X["T"], out), res(X["T"], i0), pat, op, fill, base, chm),
@@ -157,17 +165,22 @@ def build():
         return asel(out, i0, [[0, width(i0)]], A.is_gt, 0.0, 1, 0)
 
     def iota(out, pat, base, chm):
-        def f(q, X):
-            if out[0] == "pi":
-                return q.iota(res(X["T"], out), pat, base, chm)
-            return q.iota(res(X["T"], out), pat, base, chm, allow_small_or_imprecise_dtypes=True)
-        return add("g", f, [], [out], 0.16 + width(out) * CY * 2)
+        return add("g", lambda q, X: q.iota(res(X["T"], out), pat, base, chm, allow_small_or_imprecise_dtypes=True),
+                   [], [out], 0.16 + width(out) * CY * 2)
 
     nd = [0]
 
-    def dma(eng, out, i0):
+    def dmas(eng, fn, rd, wr, k):
         nd[0] += 1
-        return add(eng, lambda q, X: q.dma_start(res(X["T"], out), res(X["T"], i0)), [i0], [out], 0.08, "dma", sem="d%d" % nd[0], lat=2.2)
+        sem = "d%d" % nd[0]
+
+        def f(q, X):
+            for o, i in fn(X["T"]):
+                q.dma_start(o, i).then_inc(X["T"].sem[sem], 16)
+        return add(eng, f, rd, wr, 0.08 * k, "dma", sem=sem, lat=2.2, n=16 * k)
+
+    def dma(eng, out, i0):
+        return dmas(eng, lambda T: [(res(T, out), res(T, i0))], [i0], [out], 1)
 
     def send(dst_off, out, i0, arr, loc):
         def f(q, X):
@@ -178,249 +191,288 @@ def build():
         k = add("g", f, [i0], [], 0.4, "send", sem=loc, lat=3.0, dst=dst_off)
         add("none", None, [], [out], 0.0, "arr", sem=arr, lat=4.0, after=k, dst=-dst_off)
 
+    def xp(n0, n, side=0):
+        u = n0 // UC
+        return ap("xn", 2 * UC * u + UC * side + n0 - UC * u, n)
+
+    def pieces(n0, n):
+        return [(a, min(n0 + n, (a // UC + 1) * UC) - a) for a in range(n0, n0 + n) if a == n0 or a % UC == 0]
+
+    U0 = 256 // UC
+    NU = 1280 // UC
     dma("a", ap("us", 0, 256), ap("uses", 0, 256))
-    dma("sy", ap("xn", 0, 256), ap("piv", 0, 256))
+    dmas("sy", lambda T: [(T["xn"][:, 0:U0, 0:UC], T.piv[:, 0:256])], [], [xp(UC * u, UC) for u in range(U0)], 1)
     dma("sy", ap("s0", 0, 256), ap("safe", 0, 256))
     ones = ap("ones", 0, 128)
     memset(ones, 1.0)
-    asel(cm("I"), ones, [[-1, 128]], A.is_equal, 0.0, 0, 1)
     asel(cm("B1"), ones, [[-16, 8], [0, 16]], A.is_ge, 0.0, 0, 1)
     asel(cm("BLK"), cm("B1"), [[16, 8], [0, 16]], A.is_ge, 0.0, 15, -1)
-    asel(cm("P1"), ones, [[-1, 128]], A.is_equal, 0.0, -8, 1)
-    asel(cm("P2"), cm("P1"), [[-1, 128]], A.not_equal, 1.0, 8, 1)
-    tt(cm("PT"), cm("P2"), cm("BLK"), A.mult)
-    memset(ap("rs", 0, 2048), 0.0)
-    memset(ap("rs", 0, 128, 16), 255.0)
-    memset(ap("tab", 0, EC0), 255.0)
-    memset(ap("c256", 0, 256), 256.0)
-    memset(ap("nb", 0, 1), -1024.0)
-    memset(ap("nb", 1, 1), -1.0)
-    for nm, base, sc in (("Im1", "I", -1.0), ("Bm256", "BLK", -256.0), ("Bp256", "BLK", 256.0), ("Bm8M", "BLK", -8388608.0),
-                         ("Ip256", "I", 256.0), ("Bm2048", "BLK", -2048.0),
-                         ("Bp2048", "BLK", 2048.0), ("Bp64k", "BLK", 65536.0), ("Bm64k", "BLK", -65536.0), ("Ip512", "I", 512.0),
-                         ("Ipw", "I", 4194304.0), ("Imw", "I", -4194304.0), ("U1", "BLK", -0.5), ("Bm1", "BLK", -1.0), ("Im512", "I", -512.0),
-                         ("Im4096", "I", -4096.0), ("PT8k", "PT", 8192.0)):
-        act(cm(nm), cm(base), AF.Copy, scale=sc)
-    for nm, base, sc in (("If", "I", 1.0), ("Imf", "I", -1.0), ("PTf", "PT", 1.0), ("Bf", "BLK", 1.0)):
-        act(cf(nm), cm(base), AF.Copy, scale=sc)
+    asel(cm("I"), ones, [[-1, 128]], A.is_equal, 0.0, 0, 1)
+    asel(cm("P0"), cm("BLK"), [[-1, 128]], A.is_equal, 0.0, -8, 1)
+    asel(cm("P1"), cm("BLK"), [[-1, 128]], A.is_equal, 0.0, 8, 1)
+    asel(cm("D0"), cm("I"), [[0, 8], [-1, 16]], A.is_ge, 0.0, 7, 0)
+    asel(cm("D1"), cm("I"), [[0, 8], [1, 16]], A.is_ge, 0.0, -8, 0)
+    tt(cm("PT"), cm("P0"), cm("P1"), A.add)
+    for nm, n, k, v in (("cy", 512, 2, 2.0 ** 50), ("r16", 2048, 16, 255.0), ("r8", 2048, 8, 255.0), ("r2", 512, 2, 512.0)):
+        memset(ap(nm, 0, n), 0.0)
+        memset(ap(nm, 1 if k == 2 else 0, n // k, k), v)
+    memset(ap("tab", 0, EC), 255.0)
+    memset(ap("c8k", 0, 256), 8192.0)
+    memset(ap("nb", 0, 1), -1.0)
+    memset(ap("nb", 1, 1), 4096.0)
+    for nm, base, c in SCALED:
+        scale(cm(nm), cm(base), c)
     dma("sy", ap("us", 256, 1024), ap("uses", 256, 1024))
-    for l in range(1, 5):
-        dma("sy", ap("xn", 512 * l, 256), ap("piv", 256 * l, 256))
+    dmas("sy", lambda T: [(T["xn"][:, U0:NU, 0:UC], T.piv[:, 256:1280])], [], [xp(UC * u, UC) for u in range(U0, NU)], 1)
     dma("sy", ap("pr", 0, 160), ap("prem", 0, 160))
-    dma("sy", ap("ct", 1280, 256), ap("lem", 0, 256))
-    dma("sy", ap("ct", 1536, 256), ap("leaf", 0, 256))
+    dma("sy", ap("ct", 2560, 256), ap("lem", 0, 256))
+    dma("sy", ap("ct", 2816, 256), ap("leaf", 0, 256))
+    dmas("sy", lambda T: [(T["xn"][8 * k:8 * k + 8, :, UC:2 * UC], T.piv[8 * (k ^ 1):8 * (k ^ 1) + 8, :]) for k in range(16)],
+         [], [xp(UC * u, UC, 1) for u in range(NU)], 16)
+    c8k = ap("c8k", 0, 256)
 
-    def cl(l):
-        return float(1024 - 256 * (l - 1)) if l < 5 else 0.0
+    def layout(r, q):
+        out, c0 = [], 0
+        for n, how in KNOB["lay"][r][q]:
+            out.append((c0, n, how))
+            c0 += n
+        return out
 
-    def win(t, l):
-        return ap(t, 256 * (l - 1), EC0 + 512 * l - 256 * (l - 1)) if l < 5 else ap(t, EM0, TW - EM0)
+    def offsets(r, q, src):
+        o = 256 * (q - 1)
+        b, p = "b7", 256
+        for c0, n, how in layout(r, q):
+            if how == "n":
+                group(ap(b, p + c0, n), [("I", ap(src, o + c0, n))])
+            else:
+                ev, od = ap(src, o + c0, n // 2, 2), ap(src, o + c0 + 1, n // 2, 2)
+                group(ap(b, p + c0, n // 2), [("D0", ev), ("D1", od)])
+                group(ap(b, p + c0 + n // 2, n // 2), [("P0", ev), ("P1", od)])
+        ts(ap("of%d" % r, o, 256), ap(b, p, 256), float(MID + EC), 0.0, A.add, A.max)
 
-    for l in range(0, 5):
-        b = ap("b%d" % (4 + l % 3), 0, 256)
-        mm(b, cm("PT"), ap("xn", 512 * l, 256), True, True)
-        act(ap("xn", 512 * l + 256, 256), b, AF.Copy)
-        for q in ((1,), (2, 3, 4, 5), (), (), ())[l]:
-            o = 256 * (q - 1)
-            ts(ap("ey", o, 256), ap("us", o, 256), 1536, None, A.add)
-            ts(ap("ez", o, 256), ap("ey", o, 256), 4095, None, A.bitwise_and)
-            ts(ap("of1", o, 256), ap("ez", o, 256), cl(q), None, A.add)
-    iota(ap("ct", 0, 1280), [[0, 1280]], 0, 0)
-    iota(ap("kt", 0, EC0 + 512), [[0, EC0 + 512]], -1, 0)
-    iota(ap("idx", 0, 1024), [[1, 1024]], 7168, 0)
-    iota(ap("pi", 0, 1), [[0, 1]], 0, 1)
-    asel(cm("U2"), cm("U1"), [[1, 128]], A.is_gt, 0.0, 0, -1)
-    asel(cm("U"), cm("U2"), [[-1, 128]], A.not_equal, 0.5, 0, 1)
+    for q in (1, 2, 3, 4, 5):
+        o = 256 * (q - 1)
+        b = ap("b%d" % (4 + q % 2), 0, 256)
+        ts(ap("v1", o, 256), ap("us", o, 256), -float(MID), None, A.add)
+        group(b, [("I1520", c8k), ("Im1", c8k), ("Im16k", ap("v1", o, 256))])
+        tt(ap("e1", o, 256), ap("v1", o, 256), b, A.min)
+        offsets(1, q, "e1")
+    for k in "01":
+        iota(ap("kt" + k, 0, EC + 512), [[0, EC + 512]], 0, 0)
+        iota(ap("kt" + k, OWN, 1024), [[0, 1024]], 0, 0)
+    iota(ap("idf", 0, 1024), [[-256, 4], [1, 256]], OWN - EC - MID + 768, 0)
+    gmove(ap("idx", 0, 1024), ap("idf", 0, 1024))
+    asel(cm("B1"), cm("U1"), [[1, 128]], A.is_gt, 0.0, 0, -1)
+    asel(cm("U1"), cm("B1"), [[-1, 128]], A.not_equal, -16384.0, 0, 1)
     for i in range(16):
-        asel(ap("wm", 128 * i, 128), cm("U"), [[-16, 8], [0, 16]], A.is_equal, 0.0, -i, 1)
-    asel(cm("R"), ones, [[0, 8], [1, 16]], A.is_equal, 0.0, 0, -1)
+        asel(ap("wm", 128 * i, 128), cm("U1"), [[-16, 8], [0, 16]], A.is_equal, 0.0, -i, 1)
+    asel(cm("B1"), ones, [[0, 8], [1, 16]], A.is_equal, 0.0, 0, -1)
     for h in (0, 1):
-        mm(ap("b5", 128 * h, 128), cm("R"), cm("R"), True, True)
-    cp(ap("dq", 0, 256), ap("b5", 0, 256))
-    cp(ap("pu", 0, 160), ap("pr", 0, 160))
-    ts(ap("pj", 0, 1), ap("pi", 0, 1), 15, None, A.bitwise_and)
-    ts(ap("bias", 0, 1), ap("pj", 0, 1), -0.5, 0.5, A.mult, A.add)
-    for l in range(5):
-        ts(ap("mxn", 512 * l, 512), ap("xn", 512 * l, 512), 0.0, None, A.is_equal)
-    for q in range(1, 6):
-        cp(ap("e1", 256 * (q - 1), 256), ap("ez", 256 * (q - 1), 256))
-        if q > 1:
-            act(ap("em", 256 * (q - 1), 256), ap("e1", 256 * (q - 1), 256), AF.Relu, bias=1.0, scale=-1.0)
+        mm(ap("b5", 256 + 128 * h, 128), cm("B1"), cm("B1"), True, True)
+    scale(ap("dq", 0, 256), ap("b5", 256, 256), 1.0)
+    cp(ap("bf8", 0, 8), ap("cm", 128 * CMN.index("BLK"), 8, 16))
+    ts(ap("p1", 0, 160), ap("pr", 0, 160), 2.0, 1.0, A.mult, A.add)
+    ts(ap("p2", 0, 160), ap("pr", 0, 160), 1280.0, None, A.add)
+    tt(ap("p3", 0, 160), ap("p1", 0, 160), ap("p2", 0, 160), A.min)
+    w = UC // 16
+    for u in range(NU):
+        for side in (0, 1):
+            ts(ap("pu", 2 * w * u + w * side, w), ap("p3", 80 * side + w * u, w), -512.0 * (UC * u // 256 + 1), None, A.add)
+        ts(ap("mk", UC * u, UC), xp(UC * u, UC), 0.0, 1.0 / 128, A.is_gt, A.subtract)
+    for t in ("et2", "et3"):
+        memset(ap(t, 0, 8), NEG)
+        gmove(ap(t, 8, 256), ap("e1", 0, 256))
+    gmove(ap("et2", 264, 768), ap("e1", 256, 768))
 
-    def sa(l, k, n=256, c0=0):
-        return ap("f0", k * 256 + c0, n) if l == 0 else ap("kt", EC0 + 512 * l + k + 2 * c0, n, 2)
+    def kill(r, n0, n, k=None):
+        t, c = ("k0", 2 * n0) if n0 < 256 else ("kt%d" % (r % 2), EC + 2 * n0)
+        return ap(t, c, 2 * n) if k is None else ap(t, c + 1 - k, n, 2)
 
     cnt = [0]
 
-    def post(r, l, c0, n, how):
+    def post(r, n0, n, s):
         k = cnt[0] % 2
         cnt[0] += 1
-        XS, YZ, SS = "b%d" % k, "b%d" % (2 if how == "p" else 2 + k), "b3"
-        s = ap("s0", c0, n) if l == 0 else ap("sc%d" % (l % 3), 16 * c0 + 15, n, 16)
-        for h, a, b in ((0, "Im512", "Ip512"), (1, "Ip512", "Im512")):
-            t = [(cm("I"), ap("xn", 512 * l + 256 * h + c0, n))]
-            if r > 1:
-                t += [(cm(a), sa(l, 0, n, c0)), (cm(b), sa(l, 1, n, c0))]
-            group(ap(XS, h * n, n), t + ([(cm("Im1"), s)] if how == "p" else []))
-        v = 1024 * k
-        da, db = ap("vx", v, n), ap("vx", v + n, n)
-        f = 512 * l + 2 * c0
-        t = EC0 + 512 * l + 2 * c0
-        Y, Z = ap(YZ, 0, n), ap(YZ, n, n)
-        if how == "d":
-            xa, xb = ap(XS, 0, n), ap(XS, n, n)
-            ma, mb = ap("vx", v + 512, n), ap("vx", v + 512 + n, n)
-            tt(da, s, xa, A.is_lt)
-            tt(db, s, xb, A.is_lt)
-        else:
-            relu(ap("vx", v, 2 * n), ap(XS, 0, 2 * n))
-        group(Y, [(cm("I"), ap("c256", 0, n)), (cm("Bm256"), da)])
-        group(Z, [(cm("Bp256"), da), (cm("Bm8M"), db)])
-        if how == "d":
-            tt(ma, s, xa, A.max)
-            tt(mb, s, xb, A.max)
-            tt(ap("tab", t, n, 2), ma, Z, A.max)
-            tt(ap("tab", t + 1, n, 2), mb, Y, A.max)
-        relu(ap("fl", f, 2 * n), ap(YZ, 0, 2 * n), 1.0 / 256)
-        if how == "p":
-            group(ap(SS, 0, n, 2), [(cm("I"), s), (cm("I"), da), (cm("Ip256"), ap("fl", f + n, n))])
-            group(ap(SS, 1, n, 2), [(cm("I"), s), (cm("I"), db), (cm("Ip256"), ap("fl", f, n))])
-            move(ap("tab", t, 2 * n), ap(SS, 0, 2 * n))
+        XS, ZY = "b%d" % k, "b%d" % (2 + k)
+        for h, m, a, b in ((1, "PT", "Bmx", "Bpx"), (0, "I", "Bpx", "Bmx")):
+            for c, w_ in pieces(n0, n):
+                t = [(m, xp(c, w_))]
+                if r > 1:
+                    t += [(a, kill(r - 1, c, w_, 0)), (b, kill(r - 1, c, w_, 1))]
+                group(ap(XS, h * n + c - n0, w_), t)
+        ma, mb = ap("mx", 512 * k, n, 2), ap("mx", 512 * k + 1, n, 2)
+        Z, Y = ap(ZY, 0, n, 2), ap(ZY, 1, n, 2)
+        mm(ap(ZY, 0, 2 * n), cm("I"), ap("cy", 0, 2 * n), True, False)
+        mm(Z, cm("Bp65"), s, False, False)
+        mm(Y, cm("Bp51"), s, False, False)
+        tt(mb, s, ap(XS, n, n), A.max)
+        tt(ma, s, ap(XS, 0, n), A.max)
+        mm(Z, cm("Bm65"), mb, False, False)
+        mm(Z, cm("Bm51"), s, False, False)
+        mm(Z, cm("Bp51"), ma, False, False)
+        mm(Y, cm("Bm51"), ma, False, True)
+        return lambda: tt(ap("tab", EC + 2 * n0, 2 * n), ap("mx", 512 * k, 2 * n), ap(ZY, 0, 2 * n), A.max)
 
     def chunks(n, c):
         return [(k, min(c, n - k)) for k in range(0, n, c)]
 
+    def win(t, r, q):
+        return ap(t, 0, EC + 512 * q if r == 1 or q == 5 else OWN + 256 * (5 - q))
+
     def splice(r, q):
         o = 256 * (q - 1)
-        ein, eout = ("e1", "e2") if r == 2 else ("e2", "e3")
-        ku = "of1" if r == 2 else "eu2"
         kg = "kg%d" % q
         for k, n in chunks(256, KNOB["kch"]):
-            gather(ap(kg, 16 * k, 16 * n), win("kt", q), ap(ku, o + k, n))
-        group(ap("b4", 0, 256), [(ap("wm", 128 * i, 128), ap(kg, i, 256, 16)) for i in range(16)])
-        th, bt, e = ap("th", o, 256), ap("bt", o, 256), ap(ein, o, 256)
-        act(th, ap("b4", 0, 256), AF.Relu, bias=ap("bias", 0, 1))
-        tt(bt, th, e, A.mult)
+            either(ap(kg, 16 * k, 16 * n), ("ind", win("kt%d" % ((r - 1) % 2), r - 1, q), ap("of%d" % (r - 1), o + k, n)),
+                   1024.0, None, A.is_gt, None, AF.Relu, 1.0 / 1024, ap("nb", 0, 1))
+        t = [("I", c8k)]
+        for c0, n, how in layout(r - 1, q):
+            for i in range(16):
+                if how == "n":
+                    t.append((ap("wm", 128 * i, 128), ap(kg, 16 * c0 + i, n, 16), ap("b4", c0, n)))
+                else:
+                    d = ap("b4", c0 + i // 8, n // 2, 2)
+                    t.append((ap("wm", 128 * i, 128), ap(kg, 16 * c0 + i, n // 2, 16), d))
+                    t.append((ap("wm", 128 * (i ^ 8), 128), ap(kg, 16 * c0 + 8 * n + i, n // 2, 16), d))
+        group(ap("b4", 0, 256), t)
+        ein, eout = "e%d" % (r - 1), "e%d" % r
+        e, em = ap(ein, o, 256), ap("em", o, 256)
+        tt(em, e, ap("b4", 0, 256), A.min)
         for h in (0, 1):
-            mm(ap("b4", 256 + 128 * h, 128), ap("bt", o + 128 * h, 128), cf("Bf"), True, True)
+            group(ap("b4", 256 + 128 * h, 128), [(ap(ein, o + 128 * h, 128), cm("BLK")), (ap("em", o + 128 * h, 128), cm("Bm1"))])
         tt(ap("lt", o, 256), ap("dq", 0, 256), ap("b4", 256, 256), A.mult)
         for h in (0, 1):
-            mm(ap("b4", 8 * h, 8), ap("lt", o + 128 * h, 128), ap("cf", 128 * CFN.index("Bf"), 8, 16), True, True)
+            mm(ap("b5", 256 + 8 * h, 8), ap("lt", o + 128 * h, 128), ap("bf8", 0, 8), True, True)
         oi, ou = ap("oi", 16 * (q - 1), 16), ap("ou", 16 * (q - 1), 16)
-        ts(oi, ap("b4", 0, 16), 0.5, -1024.25, A.mult, A.add)
+        ts(oi, ap("b5", 256, 16), 0.5, (NEG + MID) / 2 - 248.25, A.mult, A.add)
         cp(ou, oi)
-        tu = ap("tu", o, 256)
-        gather(tu, ap(ein, 0, 1024), ou)
-        group(ap("b5", 0, 256), [(cm("PT8k"), th), (cm("PT8k"), ap("em", o, 256))])
-        group(ap("b6", 0, 256), [(cf("PTf"), tu), (cf("Imf"), bt)])
-        hh, sp_ = ap("hh", o, 256), ap("sp", o, 256)
-        tt(hh, tu, ap("b5", 0, 256), A.is_gt)
-        group(ap("b5", 256, 256), [(cm("BLK"), th), (cm("Bm1"), hh)])
-        relu(sp_, ap("b5", 256, 256))
-        tt(ap("b6", 256, 256), sp_, ap("b6", 0, 256), A.mult)
-        tt(ap(eout, o, 256), e, ap("b6", 256, 256), A.add)
-        if r == 2:
-            act(ap("em", o, 256), ap(eout, o, 256), AF.Relu, bias=1.0, scale=-1.0)
-        offs(r, q, eout)
+        tu, hh, t1 = ap("tu", o, 256), ap("hh", o, 256), ap("t1", o, 256)
+        gather(tu, ap("et%d" % r, 0, 8 + 256 * (q - 1)), ou, "v")
+        group(ap("b5", 0, 256), [("I", em), ("PT", tu)])
+        either(hh, ap("b5", 0, 256), 4096.0, 0.0, A.add, A.max, AF.Relu, 1.0, ap("nb", 1, 1))
+        H, Q = ap("b6", 0, 256), ap("b6", 256, 256)
+        group(H, [("Im1", c8k), ("Bp12", hh)])
+        group(Q, [("I", c8k), ("I", em), ("PT", tu), ("Bm12", hh)])
+        tt(t1, e, H, A.min)
+        tt(ap(eout, o, 256), t1, Q, A.max)
+        if r == 2 and q < 5:
+            gmove(ap("et3", 8 + o, 256), ap("e2", o, 256))
+        owner(r, q, eout)
 
-    def offs(r, q, src):
+    def owner(r, q, src):
         o = 256 * (q - 1)
-        of = ap("of%d" % r, o, 256)
         if q == 5:
-            cp(of, ap(src, o, 256))
-            if r == 2:
-                cp(ap("eu2", o, 256), of)
-            return
-        P = ap("b7", 256 * (q % 2), 256)
-        group(P, [(cf("If"), ap(src, o, 256)), (cm("Im4096"), sa(q, 0)), (cm("Im4096"), sa(q, 1))])
-        tt(ap("off", o, 256), ap("idx", o, 256), P, A.max)
-        ts(of, ap("off", o, 256), cl(q) - 8192.0, None, A.add)
-        if r == 2 and q > 1:
-            ts(ap("eu2", o, 256), ap(src, o, 256), cl(q), None, A.add)
+            return offsets(r, q, src)
+        O = ap("b7", 0, 256)
+        group(O, [("Im4", c8k), ("I", ap("idx", o, 256)), ("BLK", kill(r - 1, 256 * q, 256, 0)), ("BLK", kill(r - 1, 256 * q, 256, 1))])
+        tt(ap("eo", o, 256), ap(src, o, 256), O, A.max)
+        offsets(r, q, "eo")
 
     def sets(r, l):
         o = 256 * (l - 1)
-        c0 = 0
-        gt, sc = "gt%d" % (l % 2), "sc%d" % (l % 3)
-        for p, how in (KNOB["post"][r] if l < 5 else _D):
-            for k, n in chunks(p, KNOB["gch"]):
-                gather(ap(gt, 16 * (c0 + k), 16 * n), win("tab", l), ap("of%d" % r, o + c0 + k, n))
-            scan(ap(sc, 16 * c0, 16 * p), ap(gt, 16 * c0, 16 * p), 16 * p)
+        ga, gb, sc = "ga%d" % (l % 2), "gb%d" % (l % 2), "sc%d" % (l % 3)
+        w_, of = win("tab", r, l), "of%d" % r
+        last = []
+        for c0, n, how in layout(r, l):
+            if how == "n":
+                for k, m in chunks(n, KNOB["gch"]):
+                    gather(ap(ga, 16 * (c0 + k), 16 * m), w_, ap(of, o + c0 + k, m))
+                scan(ap(sc, 16 * c0, 16 * n), ap("r16", 0, 16 * n), ap(ga, 16 * c0, 16 * n), 255.0, A.max, A.min)
+                s = ap(sc, 16 * c0 + 15, n, 16)
+            else:
+                for k, m in chunks(n // 2, KNOB["gch"]):
+                    a = ap(ga, 16 * (c0 + k), 16 * m)
+                    gather(a, w_, ap(of, o + c0 + k, m))
+                    tt(ap(gb, 8 * c0 + 16 * k, 16 * m), ("ind", w_, ap(of, o + c0 + n // 2 + k, m)), a, A.min)
+                scan(ap(sc, 16 * c0, 8 * n), ap("r8", 0, 8 * n), ap(gb, 8 * c0, 8 * n), 255.0, A.max, A.min)
+                s = ap(sc, 16 * c0 + 7, n, 8)
             if l < 5:
-                post(r, l, c0, p, how)
-            c0 += p
-        gmove(ap("tab", o, 256) if l < 5 else ap("gs%d" % r, 0, 256), ap(sc, 15, 256, 16))
+                last.append(post(r, 256 * l + c0, n, s))
+                if r == 1:
+                    last.pop()()
+            last.append(lambda s=s, c0=c0, n=n: gmove(ap("tab", OWN + 256 * (4 - l) + c0, n) if l < 5 else ap("gs%d" % r, c0, n), s))
+        for f in last:
+            f()
 
-    def up(r, l):
-        X, PA, PB = "b%d" % (l % 2), ap("b%d" % (2 + l % 2), 0, 256), ap("b%d" % (4 + l % 2), 0, 256)
-        h = l % 2
-        mm(ap(X, 0, 256), cm("I"), ap("xn", 512 * l, 256), True, True)
-        for P, k, a, b in ((PA, 0, "Ipw", "Imw"), (PB, 256, "Imw", "Ipw")):
-            mm(P, cm("Ip512"), ap("mxn", 512 * l + k, 256), True, False)
-            c0 = 0
-            for n, how in KNOB["post" if l else "post0"][r]:
-                f = 512 * l + 2 * c0
-                mm(ap(P[0], c0, n), cm(a), ap("fl", f, n), False, False)
-                mm(ap(P[0], c0, n), cm(b), ap("fl", f + n, n), False, False)
-                c0 += n
-        w = ap("ct", 0, 1792)
-        av, bv = ap("ab", 512 * h, 256), ap("ab", 512 * h + 256, 256)
-        va, vb = ap("vv", 512 * h, 256), ap("vv", 512 * h + 256, 256)
-        ua, ub = ap("pu", 16 * l, 16), ap("pu", 80 + 16 * l, 16)
-        gather(av, w, ua, "a")
-        tt(vb, ("ind", w, ub), ap("xn", 512 * l + 256, 256), A.is_lt)
-        gather(bv, w, ub, "a")
-        mm(PA, cm("Bm2048"), vb, False, False)
-        mm(PB, cm("Bp2048"), vb, False, False)
-        tt(va, av, ap(X, 0, 256), A.is_lt)
-        mm(PA, cm("Bp64k"), va, False, True)
-        mm(PB, cm("Bm64k"), va, False, True)
-        ma, mb = ap("ma", 256 * h, 256), ap(X, 256, 256)
-        tt(ma, av, PA, A.min)
-        tt(mb, bv, PB, A.min)
-        tt(ap("ct", 256 * l, 256), ma, mb, A.max)
+    def up(r, n0):
+        k = cnt[0] % 2
+        cnt[0] += 1
+        n, l, u = UC, n0 // 256, n0 // UC
+        LIN, Q = "b%d" % k, "b%d" % (2 + k)
+        lb, la = ap(LIN, 0, n, 2), ap(LIN, 1, n, 2)
+        qb, qa = ap(Q, 0, n, 2), ap(Q, 1, n, 2)
+        t = EC + 2 * n0
+        mm(ap(LIN, 0, 2 * n), cm("Imw"), ap("tab", t, 2 * n), True, False)
+        mm(lb, cm("Ipw"), ap("tab", t + 1, n, 2), False, False)
+        mm(la, cm("Ipw"), ap("tab", t, n, 2), False, False)
+        mm(lb, cm("PT512"), ap("mk", n0, n), False, False)
+        mm(la, cm("I512"), ap("mk", n0, n), False, False)
+        mm(ap(Q, 0, 2 * n), cm("I"), ap("kt0", EC, 2 * n), True, False)
+        w_, off, x = ap("ct", 512 * (l + 1), 3072 - 512 * (l + 1)), ap("pu", 2 * w * u, 2 * w), ap("xn", 2 * UC * u, 2 * n)
+        ab, uu = ap("ab", 512 * k, 2 * n), ap("uu", 512 * k, 2 * n)
+        if KNOB["up"][r] == "L":
+            tt(uu, ("ind", w_, off), x, A.is_lt)
+            gather(ab, w_, off, "a")
+        else:
+            mm(qa, cm("I"), xp(n0, n), False, False)
+            mm(qb, cm("PT"), xp(n0, n), False, False)
+            tt(ab, ("ind", w_, off), x, A.subtract)
+            relu(uu, ab, -1.0)
+        ua, ub = ap("uu", 512 * k, n), ap("uu", 512 * k + n, n)
+        mm(lb, cm("Bp25"), ua, False, False)
+        mm(la, cm("Bm25"), ua, False, False)
+        mm(lb, cm("Bm12"), ub, False, False)
+        mm(la, cm("Bp12"), ub, False, True)
+        mm(qa, cm("I"), ap("ab", 512 * k, n), False, False)
+        mm(qb, cm("I"), ap("ab", 512 * k + n, n), False, False)
         if r < 3:
-            for k, P in ((0, PA), (1, PB)):
-                if l:
-                    act(sa(l, k), P, AF.Sign, bias=ap("nb", 0, 1))
-                else:
-                    act(sa(0, k), P, AF.Relu, bias=ap("nb", 1, 1), scale=1.0 / 1024)
+            ts(kill(r, n0, n), ap(LIN, 0, 2 * n), 0.0, 2048.0, A.max, A.min)
+        else:
+            relu(kill(r, n0, n), ap(LIN, 0, 2 * n))
+        mm(ap(Q, 0, 2 * n), cm("Im1"), kill(r, n0, n), False, True)
+        scan(ap("ct", 2 * n0, 2 * n), ap("r2", 0, 2 * n), ap(Q, 0, 2 * n), 0.0, A.min, A.max)
 
     for r in (1, 2, 3):
         if r > 1:
-            group(ap("b6", 0, 256), [(cm("Ip512"), sa(0, 0)), (cm("Ip512"), sa(0, 1))])
-            group(ap("b3", 0, 256), [(cm("I"), ap("lg%d" % (r - 1), 0, 256)), (cm("Im512"), sa(0, 0)), (cm("Im512"), sa(0, 1))])
-            tt(ap("km", 0, 256), ap("s0", 0, 256), ap("b6", 0, 256), A.min)
-            tt(ap("s0", 0, 256), ap("km", 0, 256), ap("b3", 0, 256), A.max)
+            ka, kb = kill(r - 1, 0, 256, 0), kill(r - 1, 0, 256, 1)
+            group(ap("b0", 0, 256), [("Im4", c8k), ("I", c8k), ("BLK", ka), ("BLK", kb)])
+            group(ap("b0", 256, 256), [("I", c8k), ("I", c8k), ("I", c8k), ("Bm1", ka), ("Bm1", kb)])
+            tt(ap("km", 0, 256), ap("s0", 0, 256), ap("b0", 0, 256), A.min)
+            tt(ap("b1", 0, 256), ap("lg%d" % (r - 1), 0, 256), ap("b0", 256, 256), A.min)
+            tt(ap("s0", 0, 256), ap("km", 0, 256), ap("b1", 0, 256), A.max)
         c0 = 0
-        for n, how in KNOB["post0"][r]:
-            post(r, 0, c0, n, how)
+        for n in KNOB["root"]:
+            post(r, c0, n, ap("s0", c0, n))()
             c0 += n
         if r > 1:
-            offs(r, 1, "e1")
-            if r == 2:
-                gmove(ap("e2", 0, 256), ap("e1", 0, 256))
-            for q in (2, 3, 4, 5):
+            owner(r, 1, "e1")
+            for q in (2, 3, 4):
                 splice(r, q)
         for l in (1, 2, 3, 4):
             sets(r, l)
+            if r == 3:
+                dma("sy", ap("ys", 256 * l, 256), ap("tab", OWN + 256 * (4 - l), 256))
         if r > 1:
-            gmove(ap("ct", 1280, 256), ap("lc%d" % (r - 1), 0, 256))
+            gmove(ap("ct", 2560, 256), ap("lc%d" % (r - 1), 0, 256))
+            splice(r, 5)
         sets(r, 5)
         if r < 3:
             send(1, ap("lg%d" % r, 0, 256), ap("gs%d" % r, 0, 256), "ag%d" % r, "og%d" % r)
         else:
             dma("sy", ap("ys", 0, 256), ap("s0", 0, 256))
-            dma("sy", ap("ys", 256, 1024), ap("tab", 0, 1024))
             dma("sy", ap("ys", 1280, 256), ap("gs3", 0, 256))
-        for l in (4, 3, 2, 1, 0):
-            up(r, l)
-            if r == 3 and l == 1:
-                dma("sy", ap("yc", 256, 1024), ap("ct", 256, 1024))
+        for n0 in range(1280 - UC, -1, -UC):
+            up(r, n0)
+            if r == 3 and n0 >= 256:
+                gmove(ap("ycb", n0, UC), ap("ct", 2 * n0 + 1, UC, 2))
+            if r == 3 and n0 == 256:
+                dma("sy", ap("yc", 256, 1024), ap("ycb", 256, 1024))
+            if r == 3 and n0 < 256:
+                cp(ap("ycb", n0, UC), ap("ct", 2 * n0 + 1, UC, 2))
+                dma("sy", ap("yc", n0, UC), ap("ycb", n0, UC))
         if r < 3:
-            send(-1, ap("lc%d" % r, 0, 256), ap("ct", 0, 256), "ac%d" % r, "oc%d" % r)
-        else:
-            dma("sy", ap("yc", 0, 256), ap("ct", 0, 256))
+            gmove(ap("rc%d" % r, 0, 256), ap("ct", 1, 256, 2))
+            send(-1, ap("lc%d" % r, 0, 256), ap("rc%d" % r, 0, 256), "ac%d" % r, "oc%d" % r)
     return ops
 
 
@@ -435,7 +487,7 @@ def order(ops):
     prio = [0.0] * n
     for i in range(n - 1, -1, -1):
         t = max([prio[j] for j in succ[i]] + [0.0])
-        prio[i] = t + ops[i]["cost"] + ops[i].get("lat", 0.0) + KNOB["lat"]
+        prio[i] = t + cost(ops[i], "a") + ops[i].get("lat", 0.0) + KNOB["lat"]
     npred = [len(o["deps"]) + (1 if o["kind"] == "arr" else 0) for o in ops]
     fin, place = [0.0] * n, [None] * n
     ready, free = [], {"v": 0.0, "a": 0.0, "p": 0.0, "g": 0.0, "sy": 0.0}
@@ -450,19 +502,21 @@ def order(ops):
                 t = max(t, fin[j] + KNOB["lat"])
         return t
 
+    starts = [0.0] * n
+
     def done(i, t, e):
         fin[i], place[i] = t, e
         for j in succ[i]:
             npred[j] -= 1
             if npred[j] == 0:
                 if ops[j]["kind"] == "arr":
+                    starts[j] = t
                     done(j, max(fin[ops[j]["after"]] + 1.0, when(j, "none")), "none")
                 else:
                     ready.append(j)
     for i in range(n):
         if npred[i] == 0 and ops[i]["kind"] != "arr":
             ready.append(i)
-    starts = [0.0] * n
     while ready:
         best = None
         for e in free:
@@ -476,10 +530,10 @@ def order(ops):
                     best = (key, i, e, t)
         _, i, e, t = best
         ready.remove(i)
-        free[e] = t + ops[i]["cost"]
+        free[e] = t + cost(ops[i], e)
         starts[i] = t
         queues[e].append(i)
-        done(i, t + ops[i]["cost"] + ops[i].get("lat", 0.0), e)
+        done(i, free[e] + ops[i].get("lat", 0.0), e)
     return queues, place, starts, max(fin)
 
 
@@ -513,7 +567,7 @@ def rank_program(g, core, T, topo):
     total = {}
     for i, o in enumerate(ops):
         if o["kind"] == "dma":
-            number[i] = (o["sem"], 16)
+            number[i] = (o["sem"], o["n"])
         elif o["kind"] != "c":
             other = T.cores[(rank + o["dst"]) % len(T.cores)]
             number[i] = (o["sem"], len(topo.engines(core, other) if o["kind"] == "send" else topo.engines(other, core)))
@@ -551,8 +605,8 @@ def rank_program(g, core, T, topo):
                     learn(kn, after.get((s, k), {}))
                 ins = o["fn"](Q[e], {"T": T, "topo": topo, "core": core, "rank": rank, "e": e})
                 s, k = number[i]
-                if o["kind"] != "send":
-                    ins.then_inc(T.sem[s], 1 if o["kind"] == "c" else 16)
+                if o["kind"] == "c":
+                    ins.then_inc(T.sem[s], 1)
                 after[(s, k)] = dict(kn)
                 emitted[i] = True
                 pending[e].pop(0)

@@ -6,14 +6,19 @@ TW = OWN + 1024
 MID = 1800
 NEG = -8192.0
 UC = 128
-_H = ((128, "h"), (128, "n"))
-_N = ((128, "h"), (128, "n"))
-KNOB = {"gch": 32, "kch": 32, "lat": 0.09, "self": 0.06, "pen": 0.3,
-        "lay": {1: {1: _N, 2: _H, 3: _H, 4: _H, 5: _H}, 2: {1: _H, 2: _H, 3: _H, 4: _H, 5: _H}, 3: {1: _H, 2: _H, 3: _H, 4: _H, 5: _H}},
-        "root": (128, 128), "up": {1: "L", 2: "L", 3: "L"}}
+_M = ((128, "h"), (64, "n"), (64, "n"))
+_Q = ((128, "h"), (64, "h"), (64, "n"))
+_R = ((64, "h"), (128, "h"), (64, "n"))
+_N = ((128, "n"), (128, "n"))
+KNOB = {"gch": 32, "kch": 32, "lat": 0.09, "self": 0.06, "g1": 64, "wait": 0.0, "root": (128, 128),
+        "kv": {(2, 3): 32, (3, 3): 32, (2, 2): 64, (3, 2): 64, (2, 4): 32, (3, 4): 32},
+        "av": {(2, 2): 64, (1, 4): 32, (3, 1): 16},
+        "lay": {1: {1: _M, 2: _M, 3: _M, 4: _M, 5: _N}, 2: {1: _R, 2: _Q, 3: _Q, 4: _Q, 5: _N},
+                3: {1: _R, 2: _Q, 3: ((96, 'h'), (96, 'h'), (64, 'n')), 4: ((160, 'h'), (64, 'n'), (32, 'n')), 5: _N}},
+        "lead": {'U10': 13.5, 'U20': 20.5, 'V20': 22.5, 'V30': 29, 'S25': 16, 'S35': 7, 999: 1.5, 'A21': 9.5, 'S21': 1, 'A22': 27, 'S22': 7.5, 'A23': 5.0, 'S23': 9, 'A24': 5, 'S24': 5, 'A31': 11, 'S31': 5, 'A32': 11.0, 'S32': 6, 'A33': 1.0, 'S33': 3, 'A34': 18, 'S34': 4, 'K23': 1.5, 'A11': -4, 'V21': -0.5, 'U13': -0.5, 'A14': 3, 'V11': -1.5, 'U31': -3, 'A12': 5.5, 'K33': -3.0, 'K34': -1.0, 'V34': 0.5, 'K25': -12, 'K22': -4.5, 'A15': 2.5, 'U33': -1.5, 'V35': 0.0, 'U14': 1.5, 'V31': -2.0, 'A13': 1, 'K24': 5, 'V12': 4.0, 'U22': -10.0, 'K32': -2, 'A25': -11.5, 'V24': 2.5, 'U30': -2.5, 'A35': -3.5, 'V33': 4, 'V15': -2, 'V32': 0.5, 'K35': 0.5, 'V22': 1.5, 'V23': 0.5, 'V10': -2, 'U12': -4.5, 'U24': -1.0, 'U32': -1, 'U21': -3, 'V25': -5.0, 'U11': -4, 'V14': 1.5, 'V13': -0.5}}
 
 WID = {"bfloat16": {"tab": TW, "kt0": TW, "kt1": TW, "k0": 512, "ct": 3072, "s0": 256, "km": 256, "mk": 1280,
-                    "ones": 128, "c8k": 256, "cy": 512, "r16": 2048, "r8": 2048, "r2": 512, "cm": 128 * 28, "wm": 2048,
+                    "ones": 128, "c8k": 256, "c4k": 256, "r16": 2048, "r8": 2048, "r2": 512, "cm": 128 * 32, "wm": 2048,
                     "mx": 1024, "ab": 1024, "uu": 1024, "hh": 1280, "ga0": 4096, "ga1": 4096, "gb0": 2048, "gb1": 2048,
                     "sc0": 4096, "sc1": 4096, "sc2": 4096, "kg2": 4096, "kg3": 4096, "kg4": 4096, "kg5": 4096,
                     "gs1": 256, "gs2": 256, "gs3": 256, "rc1": 256, "rc2": 256, "ycb": 1280,
@@ -35,11 +40,11 @@ SEMAPHORES = ["sv", "sa", "sp", "sg"] + ["d%d" % i for i in range(NDMA)] + [a + 
 
 A = AluOpType
 AF = ActivationFunctionType
-SCALED = (("Bm51", "BLK", -2.0 ** 51), ("Bp51", "BLK", 2.0 ** 51), ("Bp65", "BLK", 2.0 ** 65), ("Bm65", "BLK", -2.0 ** 65),
+SCALED = (("Bm34", "BLK", -2.0 ** 34), ("Bp34", "BLK", 2.0 ** 34), ("Bp48", "BLK", 2.0 ** 48), ("Bm48", "BLK", -2.0 ** 48),
           ("Im1", "I", -1.0), ("Im16k", "I", -16384.0), ("I1520", "I", 1520.0), ("U1", "BLK", 16384.0),
           ("Ipw", "I", 2.0 ** -11), ("Imw", "I", -2.0 ** -11), ("I512", "I", 512.0), ("PT512", "PT", 512.0),
-          ("Bp25", "BLK", 2.0 ** 25), ("Bm25", "BLK", -2.0 ** 25), ("Bp12", "BLK", 4096.0), ("Bm12", "BLK", -4096.0),
-          ("Bpx", "BLK", 2.0 ** -7), ("Bmx", "BLK", -2.0 ** -7), ("Bm1", "BLK", -1.0), ("Im4", "I", -4.0))
+          ("Bp17", "BLK", 2.0 ** 17), ("Bm17", "BLK", -2.0 ** 17), ("Bp12", "BLK", 4096.0), ("Bm12", "BLK", -4096.0),
+          ("Bm1", "BLK", -1.0))
 CMN = ["I", "BLK", "P0", "P1", "PT", "D0", "D1", "B1"] + [x[0] for x in SCALED]
 
 
@@ -69,7 +74,7 @@ def cost(o, e):
 
 
 def build():
-    ops, hist = [], {}
+    ops, hist, now = [], {}, [999]
     CY, GC, PC, PO = 1.04e-3, 1.62e-3, 0.5e-3, 0.025
     two = list(WID["bfloat16"]) + list(WID["uint16"]) + list(WID["float16"]) + ["xn"]
 
@@ -96,10 +101,13 @@ def build():
                 hist.setdefault(x[0], []).append((i, x[1], x[2], x[3], w))
                 if x[0] in BANKS:
                     hist[x[0]] = hist[x[0]][-70:]
-        d = {"i": i, "eng": eng, "fn": fn, "deps": deps, "cost": c, "kind": kind}
+        d = {"i": i, "eng": eng, "fn": fn, "deps": deps, "cost": c, "kind": kind, "stage": now[0]}
         d.update(kw)
         ops.append(d)
         return i
+
+    def stage(r, what, l):
+        now[0] = "%s%d%d" % (what, r, l)
 
     def tt(out, i0, i1, op):
         n = width(i1)
@@ -213,12 +221,13 @@ def build():
     asel(cm("D0"), cm("I"), [[0, 8], [-1, 16]], A.is_ge, 0.0, 7, 0)
     asel(cm("D1"), cm("I"), [[0, 8], [1, 16]], A.is_ge, 0.0, -8, 0)
     tt(cm("PT"), cm("P0"), cm("P1"), A.add)
-    for nm, n, k, v in (("cy", 512, 2, 2.0 ** 50), ("r16", 2048, 16, 255.0), ("r8", 2048, 8, 255.0), ("r2", 512, 2, 512.0)):
+    for nm, n, k, v in (("r16", 2048, 16, 255.0), ("r8", 2048, 8, 255.0), ("r2", 512, 2, 512.0)):
         memset(ap(nm, 0, n), 0.0)
         memset(ap(nm, 1 if k == 2 else 0, n // k, k), v)
     memset(ap("tab", 0, EC), 255.0)
     memset(ap("c8k", 0, 256), 8192.0)
-    memset(ap("nb", 0, 1), -1.0)
+    memset(ap("c4k", 0, 256), 4096.0)
+    memset(ap("nb", 0, 1), -1024.0)
     memset(ap("nb", 1, 1), 4096.0)
     for nm, base, c in SCALED:
         scale(cm(nm), cm(base), c)
@@ -231,17 +240,20 @@ def build():
          [], [xp(UC * u, UC, 1) for u in range(NU)], 16)
     c8k = ap("c8k", 0, 256)
 
-    def layout(r, q):
+    def layout(r, q, whole=False):
         out, c0 = [], 0
         for n, how in KNOB["lay"][r][q]:
-            out.append((c0, n, how))
+            if whole and out and out[-1][2] == how:
+                out[-1] = (out[-1][0], out[-1][1] + n, how)
+            else:
+                out.append((c0, n, how))
             c0 += n
         return out
 
     def offsets(r, q, src):
         o = 256 * (q - 1)
         b, p = "b7", 256
-        for c0, n, how in layout(r, q):
+        for c0, n, how in layout(r, q, True):
             if how == "n":
                 group(ap(b, p + c0, n), [("I", ap(src, o + c0, n))])
             else:
@@ -270,7 +282,7 @@ def build():
     for h in (0, 1):
         mm(ap("b5", 256 + 128 * h, 128), cm("B1"), cm("B1"), True, True)
     scale(ap("dq", 0, 256), ap("b5", 256, 256), 1.0)
-    cp(ap("bf8", 0, 8), ap("cm", 128 * CMN.index("BLK"), 8, 16))
+    ts(ap("bf8", 0, 8), ap("cm", 128 * CMN.index("BLK"), 8, 16), 0.5 - 2.0 ** -15, None, A.mult)
     ts(ap("p1", 0, 160), ap("pr", 0, 160), 2.0, 1.0, A.mult, A.add)
     ts(ap("p2", 0, 160), ap("pr", 0, 160), 1280.0, None, A.add)
     tt(ap("p3", 0, 160), ap("p1", 0, 160), ap("p2", 0, 160), A.min)
@@ -278,40 +290,44 @@ def build():
     for u in range(NU):
         for side in (0, 1):
             ts(ap("pu", 2 * w * u + w * side, w), ap("p3", 80 * side + w * u, w), -512.0 * (UC * u // 256 + 1), None, A.add)
-        ts(ap("mk", UC * u, UC), xp(UC * u, UC), 0.0, 1.0 / 128, A.is_gt, A.subtract)
+        ts(ap("mk", UC * u, UC), xp(UC * u, UC), 0.0, 1.0 / 128, A.is_equal, A.subtract)
     for t in ("et2", "et3"):
         memset(ap(t, 0, 8), NEG)
         gmove(ap(t, 8, 256), ap("e1", 0, 256))
     gmove(ap("et2", 264, 768), ap("e1", 256, 768))
 
-    def kill(r, n0, n, k=None):
+    def brk(r, n0, n, k=None):
         t, c = ("k0", 2 * n0) if n0 < 256 else ("kt%d" % (r % 2), EC + 2 * n0)
-        return ap(t, c, 2 * n) if k is None else ap(t, c + 1 - k, n, 2)
+        return ap(t, c, 2 * n) if k is None else ap(t, c + k, n, 2)
 
     cnt = [0]
+
+    def pivots(r, l):
+        for h, m, a, b in ((1, "PT", "I", "Im1"), (0, "I", "Im1", "I")):
+            d = ap("b%d" % (l % 2), 256 * h, 256)
+            t = [(m, xp(c, w_), ap(d[0], 256 * h + c % 256, w_)) for c, w_ in pieces(256 * l, 256)]
+            if r > 1:
+                group(d, [(a, brk(r - 1, 256 * l, 256, 0)), (b, brk(r - 1, 256 * l, 256, 1))] + t)
+            else:
+                for x in t:
+                    group(d, [x])
 
     def post(r, n0, n, s):
         k = cnt[0] % 2
         cnt[0] += 1
-        XS, ZY = "b%d" % k, "b%d" % (2 + k)
-        for h, m, a, b in ((1, "PT", "Bmx", "Bpx"), (0, "I", "Bpx", "Bmx")):
-            for c, w_ in pieces(n0, n):
-                t = [(m, xp(c, w_))]
-                if r > 1:
-                    t += [(a, kill(r - 1, c, w_, 0)), (b, kill(r - 1, c, w_, 1))]
-                group(ap(XS, h * n + c - n0, w_), t)
+        XS, ZY, c = "b%d" % (n0 // 256 % 2), "b%d" % (2 + k), n0 % 256
         ma, mb = ap("mx", 512 * k, n, 2), ap("mx", 512 * k + 1, n, 2)
         Z, Y = ap(ZY, 0, n, 2), ap(ZY, 1, n, 2)
-        mm(ap(ZY, 0, 2 * n), cm("I"), ap("cy", 0, 2 * n), True, False)
-        mm(Z, cm("Bp65"), s, False, False)
-        mm(Y, cm("Bp51"), s, False, False)
-        tt(mb, s, ap(XS, n, n), A.max)
-        tt(ma, s, ap(XS, 0, n), A.max)
-        mm(Z, cm("Bm65"), mb, False, False)
-        mm(Z, cm("Bm51"), s, False, False)
-        mm(Z, cm("Bp51"), ma, False, False)
-        mm(Y, cm("Bm51"), ma, False, True)
-        return lambda: tt(ap("tab", EC + 2 * n0, 2 * n), ap("mx", 512 * k, 2 * n), ap(ZY, 0, 2 * n), A.max)
+        mm(Y, cm("Bp17"), ap("c4k", 0, n), True, False)
+        mm(Z, cm("Bp48"), s, False, False)
+        mm(Y, cm("Bp34"), s, False, False)
+        tt(mb, s, ap(XS, 256 + c, n), A.max)
+        tt(ma, s, ap(XS, c, n), A.max)
+        mm(Z, cm("Bm48"), mb, False, False)
+        mm(Z, cm("Bm34"), s, False, False)
+        mm(Z, cm("Bp34"), ma, False, False)
+        mm(Y, cm("Bm34"), ma, False, True)
+        tt(ap("tab", EC + 2 * n0, 2 * n), ap("mx", 512 * k, 2 * n), ap(ZY, 0, 2 * n), A.max)
 
     def chunks(n, c):
         return [(k, min(c, n - k)) for k in range(0, n, c)]
@@ -322,18 +338,19 @@ def build():
     def splice(r, q):
         o = 256 * (q - 1)
         kg = "kg%d" % q
+        stage(r, "K", q)
         for k, n in chunks(256, KNOB["kch"]):
-            either(ap(kg, 16 * k, 16 * n), ("ind", win("kt%d" % ((r - 1) % 2), r - 1, q), ap("of%d" % (r - 1), o + k, n)),
-                   1024.0, None, A.is_gt, None, AF.Relu, 1.0 / 1024, ap("nb", 0, 1))
+            j = either(ap(kg, 16 * k, 16 * n), ("ind", win("kt%d" % ((r - 1) % 2), r - 1, q), ap("of%d" % (r - 1), o + k, n)),
+                       0.0, None, A.is_gt, None, AF.Sign, 1.0, 0.0)
+            ops[j]["eng"] = "v" if k < KNOB["kv"].get((r, q), 0) else "a"
+        stage(r, "S", q)
         t = [("I", c8k)]
-        for c0, n, how in layout(r - 1, q):
-            for i in range(16):
-                if how == "n":
-                    t.append((ap("wm", 128 * i, 128), ap(kg, 16 * c0 + i, n, 16), ap("b4", c0, n)))
-                else:
-                    d = ap("b4", c0 + i // 8, n // 2, 2)
-                    t.append((ap("wm", 128 * i, 128), ap(kg, 16 * c0 + i, n // 2, 16), d))
-                    t.append((ap("wm", 128 * (i ^ 8), 128), ap(kg, 16 * c0 + 8 * n + i, n // 2, 16), d))
+        for c0, n, how in layout(r - 1, q, True):
+            for p, m, x in ((0, n, 0),) if how == "n" else ((0, n // 2, 0), (n // 2, n // 2, 8)):
+                for k, j in chunks(m, KNOB["g1"] if c0 + p + m == 256 else m):
+                    for i in range(16):
+                        d = ap("b4", c0 + k, j) if how == "n" else ap("b4", c0 + 2 * k + i // 8, j, 2)
+                        t.append((ap("wm", 128 * (i ^ x), 128), ap(kg, 16 * (c0 + p + k) + i, j, 16), d))
         group(ap("b4", 0, 256), t)
         ein, eout = "e%d" % (r - 1), "e%d" % r
         e, em = ap(ein, o, 256), ap("em", o, 256)
@@ -343,112 +360,104 @@ def build():
         tt(ap("lt", o, 256), ap("dq", 0, 256), ap("b4", 256, 256), A.mult)
         for h in (0, 1):
             mm(ap("b5", 256 + 8 * h, 8), ap("lt", o + 128 * h, 128), ap("bf8", 0, 8), True, True)
-        oi, ou = ap("oi", 16 * (q - 1), 16), ap("ou", 16 * (q - 1), 16)
-        ts(oi, ap("b5", 256, 16), 0.5, (NEG + MID) / 2 - 248.25, A.mult, A.add)
-        cp(ou, oi)
+        ou = ap("ou", 16 * (q - 1), 16)
+        ts(ou, ap("b5", 256, 16), 1.5 * 2 ** 23, 1.5 * 2 ** 23 + 248 - (NEG + MID) / 2, A.add, A.subtract)
         tu, hh, t1 = ap("tu", o, 256), ap("hh", o, 256), ap("t1", o, 256)
         gather(tu, ap("et%d" % r, 0, 8 + 256 * (q - 1)), ou, "v")
+        H, Q = ap("b6", 0, 256), ap("b6", 256, 256)
         group(ap("b5", 0, 256), [("I", em), ("PT", tu)])
         either(hh, ap("b5", 0, 256), 4096.0, 0.0, A.add, A.max, AF.Relu, 1.0, ap("nb", 1, 1))
-        H, Q = ap("b6", 0, 256), ap("b6", 256, 256)
-        group(H, [("Im1", c8k), ("Bp12", hh)])
-        group(Q, [("I", c8k), ("I", em), ("PT", tu), ("Bm12", hh)])
+        group(Q, [("I", c8k), ("I", em), ("PT", tu), ("Im1", c8k, H), ("Bp12", hh, H), ("Bm12", hh)])
         tt(t1, e, H, A.min)
         tt(ap(eout, o, 256), t1, Q, A.max)
         if r == 2 and q < 5:
             gmove(ap("et3", 8 + o, 256), ap("e2", o, 256))
-        owner(r, q, eout)
+        owner(r, q, [eout])
 
     def owner(r, q, src):
         o = 256 * (q - 1)
         if q == 5:
-            return offsets(r, q, src)
+            return offsets(r, q, src[0])
         O = ap("b7", 0, 256)
-        group(O, [("Im4", c8k), ("I", ap("idx", o, 256)), ("BLK", kill(r - 1, 256 * q, 256, 0)), ("BLK", kill(r - 1, 256 * q, 256, 1))])
-        tt(ap("eo", o, 256), ap(src, o, 256), O, A.max)
+        group(O, [("BLK", brk(r - 1, 256 * q, 256, 0)), ("BLK", brk(r - 1, 256 * q, 256, 1))] + [("I", ap(x, o, 256)) for x in src])
+        tt(ap("eo", o, 256), ap("idx", o, 256), O, A.min)
         offsets(r, q, "eo")
 
     def sets(r, l):
         o = 256 * (l - 1)
         ga, gb, sc = "ga%d" % (l % 2), "gb%d" % (l % 2), "sc%d" % (l % 3)
         w_, of = win("tab", r, l), "of%d" % r
-        last = []
         for c0, n, how in layout(r, l):
             if how == "n":
+                stage(r, "A", l)
                 for k, m in chunks(n, KNOB["gch"]):
-                    gather(ap(ga, 16 * (c0 + k), 16 * m), w_, ap(of, o + c0 + k, m))
-                scan(ap(sc, 16 * c0, 16 * n), ap("r16", 0, 16 * n), ap(ga, 16 * c0, 16 * n), 255.0, A.max, A.min)
-                s = ap(sc, 16 * c0 + 15, n, 16)
+                    gather(ap(ga, 16 * (c0 + k), 16 * m), w_, ap(of, o + c0 + k, m), "a")
             else:
+                h0, nh = [x[:2] for x in layout(r, l, True) if x[0] <= c0 < x[0] + x[1]][0]
                 for k, m in chunks(n // 2, KNOB["gch"]):
-                    a = ap(ga, 16 * (c0 + k), 16 * m)
-                    gather(a, w_, ap(of, o + c0 + k, m))
-                    tt(ap(gb, 8 * c0 + 16 * k, 16 * m), ("ind", w_, ap(of, o + c0 + n // 2 + k, m)), a, A.min)
-                scan(ap(sc, 16 * c0, 8 * n), ap("r8", 0, 8 * n), ap(gb, 8 * c0, 8 * n), 255.0, A.max, A.min)
-                s = ap(sc, 16 * c0 + 7, n, 8)
+                    a, c = ap(ga, 16 * c0 + 16 * k, 16 * m), o + h0 + (c0 - h0) // 2 + k
+                    stage(r, "A", l)
+                    gather(a, w_, ap(of, c, m), "v" if (c0 - h0) // 2 + k < KNOB["av"].get((r, l), 0) else "a")
+                    stage(r, "V", l)
+                    tt(ap(gb, 8 * c0 + 16 * k, 16 * m), ("ind", w_, ap(of, c + nh // 2, m)), a, A.min)
+        stage(r, "V", l)
+        if l < 5:
+            pivots(r, l)
+        for c0, n, how in layout(r, l):
+            k, rs, g_, c = (16, "r16", ga, 16 * c0) if how == "n" else (8, "r8", gb, 8 * c0)
+            scan(ap(sc, 16 * c0, k * n), ap(rs, 0, k * n), ap(g_, c, k * n), 255.0, A.max, A.min)
+            s = ap(sc, 16 * c0 + k - 1, n, k)
             if l < 5:
-                last.append(post(r, 256 * l + c0, n, s))
-                if r == 1:
-                    last.pop()()
-            last.append(lambda s=s, c0=c0, n=n: gmove(ap("tab", OWN + 256 * (4 - l) + c0, n) if l < 5 else ap("gs%d" % r, c0, n), s))
-        for f in last:
-            f()
+                post(r, 256 * l + c0, n, s)
+            gmove(ap("tab", OWN + 256 * (4 - l) + c0, n) if l < 5 else ap("gs%d" % r, c0, n), s)
 
     def up(r, n0):
         k = cnt[0] % 2
         cnt[0] += 1
         n, l, u = UC, n0 // 256, n0 // UC
-        LIN, Q = "b%d" % k, "b%d" % (2 + k)
-        lb, la = ap(LIN, 0, n, 2), ap(LIN, 1, n, 2)
-        qb, qa = ap(Q, 0, n, 2), ap(Q, 1, n, 2)
+        k4 = cnt[0] % 4
+        P = "b%d" % k4
+        pa, pb = ap(P, 0, n, 2), ap(P, 1, n, 2)
         t = EC + 2 * n0
-        mm(ap(LIN, 0, 2 * n), cm("Imw"), ap("tab", t, 2 * n), True, False)
-        mm(lb, cm("Ipw"), ap("tab", t + 1, n, 2), False, False)
-        mm(la, cm("Ipw"), ap("tab", t, n, 2), False, False)
-        mm(lb, cm("PT512"), ap("mk", n0, n), False, False)
-        mm(la, cm("I512"), ap("mk", n0, n), False, False)
-        mm(ap(Q, 0, 2 * n), cm("I"), ap("kt0", EC, 2 * n), True, False)
+        mm(ap(P, 0, 2 * n), cm("Imw"), ap("tab", t, 2 * n), True, False)
+        mm(pa, cm("Ipw"), ap("tab", t + 1, n, 2), False, False)
+        mm(pb, cm("Ipw"), ap("tab", t, n, 2), False, False)
+        mm(pb, cm("PT512"), ap("mk", n0, n), False, False)
+        mm(pa, cm("I512"), ap("mk", n0, n), False, False)
         w_, off, x = ap("ct", 512 * (l + 1), 3072 - 512 * (l + 1)), ap("pu", 2 * w * u, 2 * w), ap("xn", 2 * UC * u, 2 * n)
-        ab, uu = ap("ab", 512 * k, 2 * n), ap("uu", 512 * k, 2 * n)
-        if KNOB["up"][r] == "L":
-            tt(uu, ("ind", w_, off), x, A.is_lt)
-            gather(ab, w_, off, "a")
-        else:
-            mm(qa, cm("I"), xp(n0, n), False, False)
-            mm(qb, cm("PT"), xp(n0, n), False, False)
-            tt(ab, ("ind", w_, off), x, A.subtract)
-            relu(uu, ab, -1.0)
+        ab, uu, mn = ap("ab", 512 * k, 2 * n), ap("uu", 512 * k, 2 * n), ap("mx", 512 * k, 2 * n)
+        tt(uu, ("ind", w_, off), x, A.is_lt)
+        gather(ab, w_, off, "a")
         ua, ub = ap("uu", 512 * k, n), ap("uu", 512 * k + n, n)
-        mm(lb, cm("Bp25"), ua, False, False)
-        mm(la, cm("Bm25"), ua, False, False)
-        mm(lb, cm("Bm12"), ub, False, False)
-        mm(la, cm("Bp12"), ub, False, True)
-        mm(qa, cm("I"), ap("ab", 512 * k, n), False, False)
-        mm(qb, cm("I"), ap("ab", 512 * k + n, n), False, False)
+        mm(pa, cm("Bp17"), ua, False, False)
+        mm(pb, cm("Bm17"), ua, False, False)
+        mm(pa, cm("Bm12"), ub, False, False)
+        mm(pb, cm("Bp12"), ub, False, True)
+        tt(ap("mx", 512 * k, n, 2), ap("ab", 512 * k, n), pa, A.min)
+        tt(ap("mx", 512 * k + 1, n, 2), ap("ab", 512 * k + n, n), pb, A.min)
+        scan(ap("ct", 2 * n0, 2 * n), ap("r2", 0, 2 * n), mn, 0.0, A.min, A.max)
         if r < 3:
-            ts(kill(r, n0, n), ap(LIN, 0, 2 * n), 0.0, 2048.0, A.max, A.min)
-        else:
-            relu(kill(r, n0, n), ap(LIN, 0, 2 * n))
-        mm(ap(Q, 0, 2 * n), cm("Im1"), kill(r, n0, n), False, True)
-        scan(ap("ct", 2 * n0, 2 * n), ap("r2", 0, 2 * n), ap(Q, 0, 2 * n), 0.0, A.min, A.max)
+            either(brk(r, n0, n), ap(P, 0, 2 * n), -1024.0, 0.0, A.add, A.max, AF.Relu, 1.0, ap("nb", 0, 1))
 
     for r in (1, 2, 3):
+        stage(r, "V", 0)
         if r > 1:
-            ka, kb = kill(r - 1, 0, 256, 0), kill(r - 1, 0, 256, 1)
-            group(ap("b0", 0, 256), [("Im4", c8k), ("I", c8k), ("BLK", ka), ("BLK", kb)])
-            group(ap("b0", 256, 256), [("I", c8k), ("I", c8k), ("I", c8k), ("Bm1", ka), ("Bm1", kb)])
-            tt(ap("km", 0, 256), ap("s0", 0, 256), ap("b0", 0, 256), A.min)
-            tt(ap("b1", 0, 256), ap("lg%d" % (r - 1), 0, 256), ap("b0", 256, 256), A.min)
-            tt(ap("s0", 0, 256), ap("km", 0, 256), ap("b1", 0, 256), A.max)
+            ka, kb = brk(r - 1, 0, 256, 0), brk(r - 1, 0, 256, 1)
+            group(ap("b6", 0, 256), [("I", ka), ("I", kb)])
+            group(ap("b6", 256, 256), [("Im1", ka), ("Im1", kb), ("I", ap("lg%d" % (r - 1), 0, 256))])
+            tt(ap("km", 0, 256), ap("s0", 0, 256), ap("b6", 0, 256), A.min)
+            tt(ap("s0", 0, 256), ap("km", 0, 256), ap("b6", 256, 256), A.max)
         c0 = 0
+        pivots(r, 0)
         for n in KNOB["root"]:
-            post(r, c0, n, ap("s0", c0, n))()
+            post(r, c0, n, ap("s0", c0, n))
             c0 += n
         if r > 1:
-            owner(r, 1, "e1")
-            for q in (2, 3, 4):
-                splice(r, q)
+            stage(r, "S", 1)
+            owner(r, 1, ["e1"])
         for l in (1, 2, 3, 4):
+            if r > 1 and l > 1:
+                splice(r, l)
             sets(r, l)
             if r == 3:
                 dma("sy", ap("ys", 256 * l, 256), ap("tab", OWN + 256 * (4 - l), 256))
@@ -462,6 +471,7 @@ def build():
             dma("sy", ap("ys", 0, 256), ap("s0", 0, 256))
             dma("sy", ap("ys", 1280, 256), ap("gs3", 0, 256))
         for n0 in range(1280 - UC, -1, -UC):
+            stage(r, "U", n0 // 256)
             up(r, n0)
             if r == 3 and n0 >= 256:
                 gmove(ap("ycb", n0, UC), ap("ct", 2 * n0 + 1, UC, 2))
@@ -478,63 +488,53 @@ def build():
 
 def order(ops):
     n = len(ops)
-    succ = [[] for _ in range(n)]
+    pred = [dict(o["deps"]) for o in ops]
     for o in ops:
-        for j in o["deps"]:
-            succ[j].append(o["i"])
         if o["kind"] == "arr":
-            succ[o["after"]].append(o["i"])
-    prio = [0.0] * n
-    for i in range(n - 1, -1, -1):
-        t = max([prio[j] for j in succ[i]] + [0.0])
-        prio[i] = t + cost(ops[i], "a") + ops[i].get("lat", 0.0) + KNOB["lat"]
-    npred = [len(o["deps"]) + (1 if o["kind"] == "arr" else 0) for o in ops]
-    fin, place = [0.0] * n, [None] * n
-    ready, free = [], {"v": 0.0, "a": 0.0, "p": 0.0, "g": 0.0, "sy": 0.0}
-    queues = {e: [] for e in free}
-
-    def when(i, e):
-        t = 0.0
-        for j, raw in ops[i]["deps"].items():
-            if place[j] == e and ops[j]["kind"] == "c":
-                t = max(t, fin[j] + (KNOB["self"] if raw and e != "p" else 0.0))
-            else:
-                t = max(t, fin[j] + KNOB["lat"])
-        return t
-
-    starts = [0.0] * n
-
-    def done(i, t, e):
-        fin[i], place[i] = t, e
-        for j in succ[i]:
-            npred[j] -= 1
-            if npred[j] == 0:
-                if ops[j]["kind"] == "arr":
-                    starts[j] = t
-                    done(j, max(fin[ops[j]["after"]] + 1.0, when(j, "none")), "none")
-                else:
-                    ready.append(j)
+            pred[o["i"]][o["after"]] = True
+    succ = [[] for _ in range(n)]
     for i in range(n):
-        if npred[i] == 0 and ops[i]["kind"] != "arr":
-            ready.append(i)
-    while ready:
-        best = None
-        for e in free:
-            for i in ready:
-                g = ops[i]["eng"]
-                if e != g and not (g == "va" and e in "va"):
-                    continue
-                t = max(free[e], when(i, e))
-                key = (t + (KNOB["pen"] if g == "va" and e == "v" and "flex" in ops[i] else 0.0), -prio[i], i)
-                if best is None or key < best[0]:
-                    best = (key, i, e, t)
-        _, i, e, t = best
-        ready.remove(i)
-        free[e] = t + cost(ops[i], e)
-        starts[i] = t
-        queues[e].append(i)
-        done(i, free[e] + ops[i].get("lat", 0.0), e)
-    return queues, place, starts, max(fin)
+        for j in pred[i]:
+            succ[j].append(i)
+    tail = [o.get("lat", 0.0) if o["kind"] != "arr" else 1.0 for o in ops]
+    plain = [o["kind"] == "c" for o in ops]
+    can = [("a", "v") if o["eng"] == "va" else (o["eng"],) for o in ops]
+    lat, own = KNOB["lat"], KNOB["self"]
+    urge = [0.0] * n
+    for i in range(n - 1, -1, -1):
+        urge[i] = max([urge[j] for j in succ[i]] + [0.0]) + cost(ops[i], "a") + tail[i] + lat
+    urge = [u + KNOB["lead"].get(o["stage"], 0.0) for u, o in zip(urge, ops)]
+    start, stop, place = [0.0] * n, [0.0] * n, [None] * n
+    free = {e: 0.0 for e in ("v", "a", "p", "g", "sy", "none")}
+    line = {e: [] for e in free}
+    ready = {e: {} for e in free}
+    left = [len(x) for x in pred]
+
+    def enter(i):
+        for e in can[i]:
+            t = 0.0
+            for j, raw in pred[i].items():
+                d = stop[j] + ((own if raw and e != "p" else 0.0) if place[j] == e and plain[j] else tail[j] + lat)
+                if d > t:
+                    t = d
+            ready[e][i] = t
+    for i in range(n):
+        if not left[i]:
+            enter(i)
+    for _ in range(n):
+        t, e = min((max(free[e], min(ready[e].values())), e) for e in free if ready[e])
+        i = max((i for i, x in ready[e].items() if x <= t + KNOB["wait"]), key=lambda i: urge[i])
+        t = max(t, ready[e][i])
+        for x in can[i]:
+            del ready[x][i]
+        start[i], stop[i], place[i] = t, t + cost(ops[i], e), e
+        free[e] = stop[i]
+        line[e].append(i)
+        for j in succ[i]:
+            left[j] -= 1
+            if not left[j]:
+                enter(j)
+    return {e: line[e] for e in line if e != "none"}, place, start, max(stop[i] + tail[i] for i in range(n))
 
 
 CACHE = {}

from concourse.mybir import dt, AluOpType, AxisListType, ActivationFunctionType

EC = 16
OWN = EC + 2560
TW = OWN + 1024
MID = 1800
NEG = -8192.0
UC = 128
_M = ((128, "h"), (64, "n"), (64, "n"))
_Q = ((128, "h"), (64, "h"), (64, "n"))
_R = ((64, "h"), (128, "h"), (64, "n"))
_N = ((128, "n"), (128, "n"))
KNOB = {"gch": 32, "kch": 32, "lat": 0.09, "self": 0.06, "g1": 64, "wait": 0.0, "root": (128, 128),
        "kv": {(2, 3): 32, (3, 3): 32, (2, 2): 64, (3, 2): 64, (2, 4): 32, (3, 4): 32},
        "av": {(2, 2): 64, (1, 4): 32, (3, 1): 16},
        "lay": {1: {1: _M, 2: _M, 3: _M, 4: _M, 5: _N}, 2: {1: _R, 2: _Q, 3: _Q, 4: _Q, 5: _N},
                3: {1: _R, 2: _Q, 3: ((96, 'h'), (96, 'h'), (64, 'n')), 4: ((160, 'h'), (64, 'n'), (32, 'n')), 5: _N}},
        "lead": {'U10': 13.5, 'U20': 20.5, 'V20': 22.5, 'V30': 29, 'S25': 16, 'S35': 7, 999: 1.5, 'A21': 9.5, 'S21': 1, 'A22': 27, 'S22': 7.5, 'A23': 5.0, 'S23': 9, 'A24': 5, 'S24': 5, 'A31': 11, 'S31': 5, 'A32': 11.0, 'S32': 6, 'A33': 1.0, 'S33': 3, 'A34': 18, 'S34': 4, 'K23': 1.5, 'A11': -4, 'V21': -0.5, 'U13': -0.5, 'A14': 3, 'V11': -1.5, 'U31': -3, 'A12': 5.5, 'K33': -3.0, 'K34': -1.0, 'V34': 0.5, 'K25': -12, 'K22': -4.5, 'A15': 2.5, 'U33': -1.5, 'V35': 0.0, 'U14': 1.5, 'V31': -2.0, 'A13': 1, 'K24': 5, 'V12': 4.0, 'U22': -10.0, 'K32': -2, 'A25': -11.5, 'V24': 2.5, 'U30': -2.5, 'A35': -3.5, 'V33': 4, 'V15': -2, 'V32': 0.5, 'K35': 0.5, 'V22': 1.5, 'V23': 0.5, 'V10': -2, 'U12': -4.5, 'U24': -1.0, 'U32': -1, 'U21': -3, 'V25': -5.0, 'U11': -4, 'V14': 1.5, 'V13': -0.5}}

WID = {"bfloat16": {"tab": TW, "kt0": TW, "kt1": TW, "k0": 512, "ct": 3072, "s0": 256, "km": 256, "mk": 1280,
                    "ones": 128, "c8k": 256, "c4k": 256, "r16": 2048, "r8": 2048, "r2": 512, "cm": 128 * 32, "wm": 2048,
                    "mx": 1024, "ab": 1024, "uu": 1024, "hh": 1280, "ga0": 4096, "ga1": 4096, "gb0": 2048, "gb1": 2048,
                    "sc0": 4096, "sc1": 4096, "sc2": 4096, "kg2": 4096, "kg3": 4096, "kg4": 4096, "kg5": 4096,
                    "gs1": 256, "gs2": 256, "gs3": 256, "rc1": 256, "rc2": 256, "ycb": 1280,
                    "lg1": 256, "lg2": 256, "lc1": 256, "lc2": 256},
       "float16": {"v1": 1280, "e1": 1280, "e2": 1280, "e3": 1280, "em": 1280, "tu": 1280, "t1": 1280, "eo": 1280, "idx": 1024},
       "float32": {"et2": 1032, "et3": 1032, "lt": 1280, "dq": 256, "bf8": 8, "nb": 2, "idf": 1024, "p1": 160, "p2": 160, "p3": 160},
       "int32": {"us": 1280, "pr": 160, "oi": 80},
       "uint16": {"pu": 160, "of1": 1280, "of2": 1280, "of3": 1280, "ou": 80}}
SCRATCH = {}
for _t in WID:
    for _n in WID[_t]:
        SCRATCH[_n] = ("sbuf", [128, WID[_t][_n]], _t)
SCRATCH["xn"] = ("sbuf", [128, 1280 // UC, 2 * UC], "bfloat16")
BANKS = ["b%d" % k for k in range(8)]
for _n in BANKS:
    SCRATCH[_n] = ("psum", [128, 512], "float32")
NDMA = 24
SEMAPHORES = ["sv", "sa", "sp", "sg"] + ["d%d" % i for i in range(NDMA)] + [a + b for a in ("ag", "ac", "og", "oc") for b in "12"]

A = AluOpType
AF = ActivationFunctionType
SCALED = (("Bm34", "BLK", -2.0 ** 34), ("Bp34", "BLK", 2.0 ** 34), ("Bp48", "BLK", 2.0 ** 48), ("Bm48", "BLK", -2.0 ** 48),
          ("Im1", "I", -1.0), ("Im16k", "I", -16384.0), ("I1520", "I", 1520.0), ("U1", "BLK", 16384.0),
          ("Ipw", "I", 2.0 ** -11), ("Imw", "I", -2.0 ** -11), ("I512", "I", 512.0), ("PT512", "PT", 512.0),
          ("Bp17", "BLK", 2.0 ** 17), ("Bm17", "BLK", -2.0 ** 17), ("Bp12", "BLK", 4096.0), ("Bm12", "BLK", -4096.0),
          ("Bm1", "BLK", -1.0))
CMN = ["I", "BLK", "P0", "P1", "PT", "D0", "D1", "B1"] + [x[0] for x in SCALED]


def ap(name, lo, n, step=1):
    return (name, lo, lo + (n - 1) * step + 1, step)


def res(T, a):
    if a[0] == "ind":
        return res(T, a[1]).indirect(res(T, a[2]))
    if a[0] == "xn":
        u = a[1] // (2 * UC)
        return T["xn"][:, u, a[1] - 2 * UC * u:a[2] - 2 * UC * u]
    return T[a[0]][:, a[1]:a[2]] if a[3] == 1 else T[a[0]][:, a[1]:a[2]:a[3]]


def cm(n):
    return ap("cm", 128 * CMN.index(n), 128)


def width(a):
    return (a[2] - a[1] + a[3] - 1) // a[3]


def cost(o, e):
    return o["cost"][e] if isinstance(o["cost"], dict) else o["cost"]


def build():
    ops, hist, now = [], {}, [999]
    CY, GC, PC, PO = 1.04e-3, 1.62e-3, 0.5e-3, 0.025
    two = list(WID["bfloat16"]) + list(WID["uint16"]) + list(WID["float16"]) + ["xn"]

    def regs(a):
        return [a[1], a[2]] if a[0] == "ind" else [a]

    def add(eng, fn, rd, wr, c, kind="c", **kw):
        i = len(ops)
        deps = {}
        rr = [x for a in rd for x in regs(a)]
        ww = [x for a in wr for x in regs(a)]
        for w, xs in ((False, rr), (True, ww)):
            for nm, lo, hi, st in xs:
                for (j, l2, h2, s2, w2) in hist.get(nm, []):
                    if lo < h2 and l2 < hi and (w or w2) and not (st == s2 and (lo - l2) % st):
                        deps[j] = True
                    elif nm in BANKS:
                        deps.setdefault(j, False)
        for x in ww:
            if x[0] not in BANKS and x[3] == 1:
                hist[x[0]] = [e for e in hist.get(x[0], []) if not (x[1] <= e[1] and e[2] <= x[2])]
        for w, xs in ((False, rr), (True, ww)):
            for x in xs:
                hist.setdefault(x[0], []).append((i, x[1], x[2], x[3], w))
                if x[0] in BANKS:
                    hist[x[0]] = hist[x[0]][-70:]
        d = {"i": i, "eng": eng, "fn": fn, "deps": deps, "cost": c, "kind": kind, "stage": now[0]}
        d.update(kw)
        ops.append(d)
        return i

    def stage(r, what, l):
        now[0] = "%s%d%d" % (what, r, l)

    def tt(out, i0, i1, op):
        n = width(i1)
        c = n * GC if i0[0] == "ind" else n * CY * (1 if i0[0] in BANKS or i1[0] in BANKS else 2)
        return add("v", lambda q, X: q.tensor_tensor(res(X["T"], out), res(X["T"], i0), res(X["T"], i1), op), [i0, i1], [out], 0.06 + c)

    def half(out, i0):
        return 0.06 + width(i0) * CY * (0.5 if out[0] in two and i0[0] in two else 1)

    def ts(out, i0, s1, s2, o1, o2=None):
        def f(q, X):
            a, b = res(X["T"], out), res(X["T"], i0)
            return q.tensor_scalar(a, b, s1, None, o1) if o2 is None else q.tensor_scalar(a, b, s1, s2, o1, o2)
        return add("v", f, [i0], [out], half(out, i0))

    def cp(out, i0):
        return add("v", lambda q, X: q.tensor_copy(res(X["T"], out), res(X["T"], i0)), [i0], [out], half(out, i0))

    def scan(out, d0, d1, first, o0, o1):
        return add("v", lambda q, X: q.tensor_tensor_scan(res(X["T"], out), res(X["T"], d0), res(X["T"], d1), first, o0, o1),
                   [d0, d1], [out], half(out, d1))

    def memset(out, v):
        return add("v", lambda q, X: q.memset(res(X["T"], out), v), [], [out], 0.06 + width(out) * CY * (0.5 if out[0] in two else 1))

    def either(out, i0, s1, s2, o1, o2, func, scale, bias):
        def f(q, X):
            a, b = res(X["T"], out), res(X["T"], i0)
            if X["e"] == "v":
                if o1 is None:
                    return q.tensor_copy(a, b)
                return q.tensor_scalar(a, b, s1, None, o1) if o2 is None else q.tensor_scalar(a, b, s1, s2, o1, o2)
            return q.activation(a, b, func, bias=res(X["T"], bias) if isinstance(bias, tuple) else bias, scale=scale)
        rd = [i0] + [x for x in (bias,) if isinstance(x, tuple)]
        if i0[0] == "ind":
            return add("va", f, rd, [out], 0.06 + width(out) * GC, flex=True)
        return add("va", f, rd, [out], {"v": half(out, i0), "a": 0.065 + width(i0) * CY})

    def scale(out, i0, c):
        return either(out, i0, c, None, A.mult, None, AF.Copy, c, 0.0)

    def relu(out, i0, c=1.0):
        return either(out, i0, c, 0.0, A.mult, A.max, AF.Relu, c, 0.0)

    def gather(out, win, off, eng="va"):
        k = either(out, ("ind", win, off), None, None, None, None, AF.Copy, 1.0, 0.0)
        ops[k]["eng"] = eng
        return k

    def mm(out, lt, rhs, st, sp_):
        c = PO + max(64, width(rhs)) * PC * (4 if lt[0] == "lt" else 1)
        return add("p", lambda q, X: q.matmul(res(X["T"], out), res(X["T"], lt), res(X["T"], rhs), st, sp_), [lt, rhs], [out], c)

    def group(out, terms):
        for k, t in enumerate(terms):
            mm(t[2] if len(t) > 2 else out, cm(t[0]) if isinstance(t[0], str) else t[0], t[1], k == 0, k == len(terms) - 1)

    def asel(out, i0, pat, op, fill, base, chm):
        return add("g", lambda q, X: q.affine_select(res(X["T"], out), res(X["T"], i0), pat, op, fill, base, chm),
                   [i0], [out], 0.2 + width(out) * CY * 2)

    def gmove(out, i0):
        return asel(out, i0, [[0, width(i0)]], A.is_gt, 0.0, 1, 0)

    def iota(out, pat, base, chm):
        return add("g", lambda q, X: q.iota(res(X["T"], out), pat, base, chm, allow_small_or_imprecise_dtypes=True),
                   [], [out], 0.16 + width(out) * CY * 2)

    nd = [0]

    def dmas(eng, fn, rd, wr, k):
        nd[0] += 1
        sem = "d%d" % nd[0]

        def f(q, X):
            for o, i in fn(X["T"]):
                q.dma_start(o, i).then_inc(X["T"].sem[sem], 16)
        return add(eng, f, rd, wr, 0.08 * k, "dma", sem=sem, lat=2.2, n=16 * k)

    def dma(eng, out, i0):
        return dmas(eng, lambda T: [(res(T, out), res(T, i0))], [i0], [out], 1)

    def send(dst_off, out, i0, arr, loc):
        def f(q, X):
            topo, T, core = X["topo"], X["T"], X["core"]
            dst = T.cores[(X["rank"] + dst_off) % len(T.cores)]
            rid, pid = topo.addr(dst, core)
            q.remote_dma(res(T, out), res(T, i0), T.sem[arr], T.sem[loc], pid, rid, topo.mask(core, dst))
        k = add("g", f, [i0], [], 0.4, "send", sem=loc, lat=3.0, dst=dst_off)
        add("none", None, [], [out], 0.0, "arr", sem=arr, lat=4.0, after=k, dst=-dst_off)

    def xp(n0, n, side=0):
        u = n0 // UC
        return ap("xn", 2 * UC * u + UC * side + n0 - UC * u, n)

    def pieces(n0, n):
        return [(a, min(n0 + n, (a // UC + 1) * UC) - a) for a in range(n0, n0 + n) if a == n0 or a % UC == 0]

    U0 = 256 // UC
    NU = 1280 // UC
    dma("a", ap("us", 0, 256), ap("uses", 0, 256))
    dmas("sy", lambda T: [(T["xn"][:, 0:U0, 0:UC], T.piv[:, 0:256])], [], [xp(UC * u, UC) for u in range(U0)], 1)
    dma("sy", ap("s0", 0, 256), ap("safe", 0, 256))
    ones = ap("ones", 0, 128)
    memset(ones, 1.0)
    asel(cm("B1"), ones, [[-16, 8], [0, 16]], A.is_ge, 0.0, 0, 1)
    asel(cm("BLK"), cm("B1"), [[16, 8], [0, 16]], A.is_ge, 0.0, 15, -1)
    asel(cm("I"), ones, [[-1, 128]], A.is_equal, 0.0, 0, 1)
    asel(cm("P0"), cm("BLK"), [[-1, 128]], A.is_equal, 0.0, -8, 1)
    asel(cm("P1"), cm("BLK"), [[-1, 128]], A.is_equal, 0.0, 8, 1)
    asel(cm("D0"), cm("I"), [[0, 8], [-1, 16]], A.is_ge, 0.0, 7, 0)
    asel(cm("D1"), cm("I"), [[0, 8], [1, 16]], A.is_ge, 0.0, -8, 0)
    tt(cm("PT"), cm("P0"), cm("P1"), A.add)
    for nm, n, k, v in (("r16", 2048, 16, 255.0), ("r8", 2048, 8, 255.0), ("r2", 512, 2, 512.0)):
        memset(ap(nm, 0, n), 0.0)
        memset(ap(nm, 1 if k == 2 else 0, n // k, k), v)
    memset(ap("tab", 0, EC), 255.0)
    memset(ap("c8k", 0, 256), 8192.0)
    memset(ap("c4k", 0, 256), 4096.0)
    memset(ap("nb", 0, 1), -1024.0)
    memset(ap("nb", 1, 1), 4096.0)
    for nm, base, c in SCALED:
        scale(cm(nm), cm(base), c)
    dma("sy", ap("us", 256, 1024), ap("uses", 256, 1024))
    dmas("sy", lambda T: [(T["xn"][:, U0:NU, 0:UC], T.piv[:, 256:1280])], [], [xp(UC * u, UC) for u in range(U0, NU)], 1)
    dma("sy", ap("pr", 0, 160), ap("prem", 0, 160))
    dma("sy", ap("ct", 2560, 256), ap("lem", 0, 256))
    dma("sy", ap("ct", 2816, 256), ap("leaf", 0, 256))
    dmas("sy", lambda T: [(T["xn"][8 * k:8 * k + 8, :, UC:2 * UC], T.piv[8 * (k ^ 1):8 * (k ^ 1) + 8, :]) for k in range(16)],
         [], [xp(UC * u, UC, 1) for u in range(NU)], 16)
    c8k = ap("c8k", 0, 256)

    def layout(r, q, whole=False):
        out, c0 = [], 0
        for n, how in KNOB["lay"][r][q]:
            if whole and out and out[-1][2] == how:
                out[-1] = (out[-1][0], out[-1][1] + n, how)
            else:
                out.append((c0, n, how))
            c0 += n
        return out

    def offsets(r, q, src):
        o = 256 * (q - 1)
        b, p = "b7", 256
        for c0, n, how in layout(r, q, True):
            if how == "n":
                group(ap(b, p + c0, n), [("I", ap(src, o + c0, n))])
            else:
                ev, od = ap(src, o + c0, n // 2, 2), ap(src, o + c0 + 1, n // 2, 2)
                group(ap(b, p + c0, n // 2), [("D0", ev), ("D1", od)])
                group(ap(b, p + c0 + n // 2, n // 2), [("P0", ev), ("P1", od)])
        ts(ap("of%d" % r, o, 256), ap(b, p, 256), float(MID + EC), 0.0, A.add, A.max)

    for q in (1, 2, 3, 4, 5):
        o = 256 * (q - 1)
        b = ap("b%d" % (4 + q % 2), 0, 256)
        ts(ap("v1", o, 256), ap("us", o, 256), -float(MID), None, A.add)
        group(b, [("I1520", c8k), ("Im1", c8k), ("Im16k", ap("v1", o, 256))])
        tt(ap("e1", o, 256), ap("v1", o, 256), b, A.min)
        offsets(1, q, "e1")
    for k in "01":
        iota(ap("kt" + k, 0, EC + 512), [[0, EC + 512]], 0, 0)
        iota(ap("kt" + k, OWN, 1024), [[0, 1024]], 0, 0)
    iota(ap("idf", 0, 1024), [[-256, 4], [1, 256]], OWN - EC - MID + 768, 0)
    gmove(ap("idx", 0, 1024), ap("idf", 0, 1024))
    asel(cm("B1"), cm("U1"), [[1, 128]], A.is_gt, 0.0, 0, -1)
    asel(cm("U1"), cm("B1"), [[-1, 128]], A.not_equal, -16384.0, 0, 1)
    for i in range(16):
        asel(ap("wm", 128 * i, 128), cm("U1"), [[-16, 8], [0, 16]], A.is_equal, 0.0, -i, 1)
    asel(cm("B1"), ones, [[0, 8], [1, 16]], A.is_equal, 0.0, 0, -1)
    for h in (0, 1):
        mm(ap("b5", 256 + 128 * h, 128), cm("B1"), cm("B1"), True, True)
    scale(ap("dq", 0, 256), ap("b5", 256, 256), 1.0)
    ts(ap("bf8", 0, 8), ap("cm", 128 * CMN.index("BLK"), 8, 16), 0.5 - 2.0 ** -15, None, A.mult)
    ts(ap("p1", 0, 160), ap("pr", 0, 160), 2.0, 1.0, A.mult, A.add)
    ts(ap("p2", 0, 160), ap("pr", 0, 160), 1280.0, None, A.add)
    tt(ap("p3", 0, 160), ap("p1", 0, 160), ap("p2", 0, 160), A.min)
    w = UC // 16
    for u in range(NU):
        for side in (0, 1):
            ts(ap("pu", 2 * w * u + w * side, w), ap("p3", 80 * side + w * u, w), -512.0 * (UC * u // 256 + 1), None, A.add)
        ts(ap("mk", UC * u, UC), xp(UC * u, UC), 0.0, 1.0 / 128, A.is_equal, A.subtract)
    for t in ("et2", "et3"):
        memset(ap(t, 0, 8), NEG)
        gmove(ap(t, 8, 256), ap("e1", 0, 256))
    gmove(ap("et2", 264, 768), ap("e1", 256, 768))

    def brk(r, n0, n, k=None):
        t, c = ("k0", 2 * n0) if n0 < 256 else ("kt%d" % (r % 2), EC + 2 * n0)
        return ap(t, c, 2 * n) if k is None else ap(t, c + k, n, 2)

    cnt = [0]

    def pivots(r, l):
        for h, m, a, b in ((1, "PT", "I", "Im1"), (0, "I", "Im1", "I")):
            d = ap("b%d" % (l % 2), 256 * h, 256)
            t = [(m, xp(c, w_), ap(d[0], 256 * h + c % 256, w_)) for c, w_ in pieces(256 * l, 256)]
            if r > 1:
                group(d, [(a, brk(r - 1, 256 * l, 256, 0)), (b, brk(r - 1, 256 * l, 256, 1))] + t)
            else:
                for x in t:
                    group(d, [x])

    def post(r, n0, n, s):
        k = cnt[0] % 2
        cnt[0] += 1
        XS, ZY, c = "b%d" % (n0 // 256 % 2), "b%d" % (2 + k), n0 % 256
        ma, mb = ap("mx", 512 * k, n, 2), ap("mx", 512 * k + 1, n, 2)
        Z, Y = ap(ZY, 0, n, 2), ap(ZY, 1, n, 2)
        mm(Y, cm("Bp17"), ap("c4k", 0, n), True, False)
        mm(Z, cm("Bp48"), s, False, False)
        mm(Y, cm("Bp34"), s, False, False)
        tt(mb, s, ap(XS, 256 + c, n), A.max)
        tt(ma, s, ap(XS, c, n), A.max)
        mm(Z, cm("Bm48"), mb, False, False)
        mm(Z, cm("Bm34"), s, False, False)
        mm(Z, cm("Bp34"), ma, False, False)
        mm(Y, cm("Bm34"), ma, False, True)
        tt(ap("tab", EC + 2 * n0, 2 * n), ap("mx", 512 * k, 2 * n), ap(ZY, 0, 2 * n), A.max)

    def chunks(n, c):
        return [(k, min(c, n - k)) for k in range(0, n, c)]

    def win(t, r, q):
        return ap(t, 0, EC + 512 * q if r == 1 or q == 5 else OWN + 256 * (5 - q))

    def splice(r, q):
        o = 256 * (q - 1)
        kg = "kg%d" % q
        stage(r, "K", q)
        for k, n in chunks(256, KNOB["kch"]):
            j = either(ap(kg, 16 * k, 16 * n), ("ind", win("kt%d" % ((r - 1) % 2), r - 1, q), ap("of%d" % (r - 1), o + k, n)),
                       0.0, None, A.is_gt, None, AF.Sign, 1.0, 0.0)
            ops[j]["eng"] = "v" if k < KNOB["kv"].get((r, q), 0) else "a"
        stage(r, "S", q)
        t = [("I", c8k)]
        for c0, n, how in layout(r - 1, q, True):
            for p, m, x in ((0, n, 0),) if how == "n" else ((0, n // 2, 0), (n // 2, n // 2, 8)):
                for k, j in chunks(m, KNOB["g1"] if c0 + p + m == 256 else m):
                    for i in range(16):
                        d = ap("b4", c0 + k, j) if how == "n" else ap("b4", c0 + 2 * k + i // 8, j, 2)
                        t.append((ap("wm", 128 * (i ^ x), 128), ap(kg, 16 * (c0 + p + k) + i, j, 16), d))
        group(ap("b4", 0, 256), t)
        ein, eout = "e%d" % (r - 1), "e%d" % r
        e, em = ap(ein, o, 256), ap("em", o, 256)
        tt(em, e, ap("b4", 0, 256), A.min)
        for h in (0, 1):
            group(ap("b4", 256 + 128 * h, 128), [(ap(ein, o + 128 * h, 128), cm("BLK")), (ap("em", o + 128 * h, 128), cm("Bm1"))])
        tt(ap("lt", o, 256), ap("dq", 0, 256), ap("b4", 256, 256), A.mult)
        for h in (0, 1):
            mm(ap("b5", 256 + 8 * h, 8), ap("lt", o + 128 * h, 128), ap("bf8", 0, 8), True, True)
        ou = ap("ou", 16 * (q - 1), 16)
        ts(ou, ap("b5", 256, 16), 1.5 * 2 ** 23, 1.5 * 2 ** 23 + 248 - (NEG + MID) / 2, A.add, A.subtract)
        tu, hh, t1 = ap("tu", o, 256), ap("hh", o, 256), ap("t1", o, 256)
        gather(tu, ap("et%d" % r, 0, 8 + 256 * (q - 1)), ou, "v")
        H, Q = ap("b6", 0, 256), ap("b6", 256, 256)
        group(ap("b5", 0, 256), [("I", em), ("PT", tu)])
        either(hh, ap("b5", 0, 256), 4096.0, 0.0, A.add, A.max, AF.Relu, 1.0, ap("nb", 1, 1))
        group(Q, [("I", c8k), ("I", em), ("PT", tu), ("Im1", c8k, H), ("Bp12", hh, H), ("Bm12", hh)])
        tt(t1, e, H, A.min)
        tt(ap(eout, o, 256), t1, Q, A.max)
        if r == 2 and q < 5:
            gmove(ap("et3", 8 + o, 256), ap("e2", o, 256))
        owner(r, q, [eout])

    def owner(r, q, src):
        o = 256 * (q - 1)
        if q == 5:
            return offsets(r, q, src[0])
        O = ap("b7", 0, 256)
        group(O, [("BLK", brk(r - 1, 256 * q, 256, 0)), ("BLK", brk(r - 1, 256 * q, 256, 1))] + [("I", ap(x, o, 256)) for x in src])
        tt(ap("eo", o, 256), ap("idx", o, 256), O, A.min)
        offsets(r, q, "eo")

    def sets(r, l):
        o = 256 * (l - 1)
        ga, gb, sc = "ga%d" % (l % 2), "gb%d" % (l % 2), "sc%d" % (l % 3)
        w_, of = win("tab", r, l), "of%d" % r
        for c0, n, how in layout(r, l):
            if how == "n":
                stage(r, "A", l)
                for k, m in chunks(n, KNOB["gch"]):
                    gather(ap(ga, 16 * (c0 + k), 16 * m), w_, ap(of, o + c0 + k, m), "a")
            else:
                h0, nh = [x[:2] for x in layout(r, l, True) if x[0] <= c0 < x[0] + x[1]][0]
                for k, m in chunks(n // 2, KNOB["gch"]):
                    a, c = ap(ga, 16 * c0 + 16 * k, 16 * m), o + h0 + (c0 - h0) // 2 + k
                    stage(r, "A", l)
                    gather(a, w_, ap(of, c, m), "v" if (c0 - h0) // 2 + k < KNOB["av"].get((r, l), 0) else "a")
                    stage(r, "V", l)
                    tt(ap(gb, 8 * c0 + 16 * k, 16 * m), ("ind", w_, ap(of, c + nh // 2, m)), a, A.min)
        stage(r, "V", l)
        if l < 5:
            pivots(r, l)
        for c0, n, how in layout(r, l):
            k, rs, g_, c = (16, "r16", ga, 16 * c0) if how == "n" else (8, "r8", gb, 8 * c0)
            scan(ap(sc, 16 * c0, k * n), ap(rs, 0, k * n), ap(g_, c, k * n), 255.0, A.max, A.min)
            s = ap(sc, 16 * c0 + k - 1, n, k)
            if l < 5:
                post(r, 256 * l + c0, n, s)
            gmove(ap("tab", OWN + 256 * (4 - l) + c0, n) if l < 5 else ap("gs%d" % r, c0, n), s)

    def up(r, n0):
        k = cnt[0] % 2
        cnt[0] += 1
        n, l, u = UC, n0 // 256, n0 // UC
        k4 = cnt[0] % 4
        P = "b%d" % k4
        pa, pb = ap(P, 0, n, 2), ap(P, 1, n, 2)
        t = EC + 2 * n0
        mm(ap(P, 0, 2 * n), cm("Imw"), ap("tab", t, 2 * n), True, False)
        mm(pa, cm("Ipw"), ap("tab", t + 1, n, 2), False, False)
        mm(pb, cm("Ipw"), ap("tab", t, n, 2), False, False)
        mm(pb, cm("PT512"), ap("mk", n0, n), False, False)
        mm(pa, cm("I512"), ap("mk", n0, n), False, False)
        w_, off, x = ap("ct", 512 * (l + 1), 3072 - 512 * (l + 1)), ap("pu", 2 * w * u, 2 * w), ap("xn", 2 * UC * u, 2 * n)
        ab, uu, mn = ap("ab", 512 * k, 2 * n), ap("uu", 512 * k, 2 * n), ap("mx", 512 * k, 2 * n)
        tt(uu, ("ind", w_, off), x, A.is_lt)
        gather(ab, w_, off, "a")
        ua, ub = ap("uu", 512 * k, n), ap("uu", 512 * k + n, n)
        mm(pa, cm("Bp17"), ua, False, False)
        mm(pb, cm("Bm17"), ua, False, False)
        mm(pa, cm("Bm12"), ub, False, False)
        mm(pb, cm("Bp12"), ub, False, True)
        tt(ap("mx", 512 * k, n, 2), ap("ab", 512 * k, n), pa, A.min)
        tt(ap("mx", 512 * k + 1, n, 2), ap("ab", 512 * k + n, n), pb, A.min)
        scan(ap("ct", 2 * n0, 2 * n), ap("r2", 0, 2 * n), mn, 0.0, A.min, A.max)
        if r < 3:
            either(brk(r, n0, n), ap(P, 0, 2 * n), -1024.0, 0.0, A.add, A.max, AF.Relu, 1.0, ap("nb", 0, 1))

    for r in (1, 2, 3):
        stage(r, "V", 0)
        if r > 1:
            ka, kb = brk(r - 1, 0, 256, 0), brk(r - 1, 0, 256, 1)
            group(ap("b6", 0, 256), [("I", ka), ("I", kb)])
            group(ap("b6", 256, 256), [("Im1", ka), ("Im1", kb), ("I", ap("lg%d" % (r - 1), 0, 256))])
            tt(ap("km", 0, 256), ap("s0", 0, 256), ap("b6", 0, 256), A.min)
            tt(ap("s0", 0, 256), ap("km", 0, 256), ap("b6", 256, 256), A.max)
        c0 = 0
        pivots(r, 0)
        for n in KNOB["root"]:
            post(r, c0, n, ap("s0", c0, n))
            c0 += n
        if r > 1:
            stage(r, "S", 1)
            owner(r, 1, ["e1"])
        for l in (1, 2, 3, 4):
            if r > 1 and l > 1:
                splice(r, l)
            sets(r, l)
            if r == 3:
                dma("sy", ap("ys", 256 * l, 256), ap("tab", OWN + 256 * (4 - l), 256))
        if r > 1:
            gmove(ap("ct", 2560, 256), ap("lc%d" % (r - 1), 0, 256))
            splice(r, 5)
        sets(r, 5)
        if r < 3:
            send(1, ap("lg%d" % r, 0, 256), ap("gs%d" % r, 0, 256), "ag%d" % r, "og%d" % r)
        else:
            dma("sy", ap("ys", 0, 256), ap("s0", 0, 256))
            dma("sy", ap("ys", 1280, 256), ap("gs3", 0, 256))
        for n0 in range(1280 - UC, -1, -UC):
            stage(r, "U", n0 // 256)
            up(r, n0)
            if r == 3 and n0 >= 256:
                gmove(ap("ycb", n0, UC), ap("ct", 2 * n0 + 1, UC, 2))
            if r == 3 and n0 == 256:
                dma("sy", ap("yc", 256, 1024), ap("ycb", 256, 1024))
            if r == 3 and n0 < 256:
                cp(ap("ycb", n0, UC), ap("ct", 2 * n0 + 1, UC, 2))
                dma("sy", ap("yc", n0, UC), ap("ycb", n0, UC))
        if r < 3:
            gmove(ap("rc%d" % r, 0, 256), ap("ct", 1, 256, 2))
            send(-1, ap("lc%d" % r, 0, 256), ap("rc%d" % r, 0, 256), "ac%d" % r, "oc%d" % r)
    return ops


def order(ops):
    n = len(ops)
    pred = [dict(o["deps"]) for o in ops]
    for o in ops:
        if o["kind"] == "arr":
            pred[o["i"]][o["after"]] = True
    succ = [[] for _ in range(n)]
    for i in range(n):
        for j in pred[i]:
            succ[j].append(i)
    tail = [o.get("lat", 0.0) if o["kind"] != "arr" else 1.0 for o in ops]
    plain = [o["kind"] == "c" for o in ops]
    can = [("a", "v") if o["eng"] == "va" else (o["eng"],) for o in ops]
    lat, own = KNOB["lat"], KNOB["self"]
    urge = [0.0] * n
    for i in range(n - 1, -1, -1):
        urge[i] = max([urge[j] for j in succ[i]] + [0.0]) + cost(ops[i], "a") + tail[i] + lat
    urge = [u + KNOB["lead"].get(o["stage"], 0.0) for u, o in zip(urge, ops)]
    start, stop, place = [0.0] * n, [0.0] * n, [None] * n
    free = {e: 0.0 for e in ("v", "a", "p", "g", "sy", "none")}
    line = {e: [] for e in free}
    ready = {e: {} for e in free}
    left = [len(x) for x in pred]

    def enter(i):
        for e in can[i]:
            t = 0.0
            for j, raw in pred[i].items():
                d = stop[j] + ((own if raw and e != "p" else 0.0) if place[j] == e and plain[j] else tail[j] + lat)
                if d > t:
                    t = d
            ready[e][i] = t
    for i in range(n):
        if not left[i]:
            enter(i)
    for _ in range(n):
        t, e = min((max(free[e], min(ready[e].values())), e) for e in free if ready[e])
        i = max((i for i, x in ready[e].items() if x <= t + KNOB["wait"]), key=lambda i: urge[i])
        t = max(t, ready[e][i])
        for x in can[i]:
            del ready[x][i]
        start[i], stop[i], place[i] = t, t + cost(ops[i], e), e
        free[e] = stop[i]
        line[e].append(i)
        for j in succ[i]:
            left[j] -= 1
            if not left[j]:
                enter(j)
    return {e: line[e] for e in line if e != "none"}, place, start, max(stop[i] + tail[i] for i in range(n))


CACHE = {}


def plan():
    if "p" not in CACHE:
        ops = build()
        q, place, starts, end = order(ops)
        CACHE["p"] = (ops, q, place, starts, end)
    return CACHE["p"]


SEM = {"v": "sv", "a": "sa", "p": "sp", "g": "sg"}


def rank_program(g, core, T, topo):
    rank = T.rank_of(core)
    if rank is None:
        return
    ops, queues, place, starts, end = plan()
    Q = {"v": g.vector, "a": g.scalar, "p": g.tensor, "g": g, "sy": g.sync}
    number = {}
    for e in queues:
        k = 0
        for i in queues[e]:
            if ops[i]["kind"] == "c":
                k += 1
                number[i] = (SEM[e], k)
    total = {}
    for i, o in enumerate(ops):
        if o["kind"] == "dma":
            number[i] = (o["sem"], o["n"])
        elif o["kind"] != "c":
            other = T.cores[(rank + o["dst"]) % len(T.cores)]
            number[i] = (o["sem"], len(topo.engines(core, other) if o["kind"] == "send" else topo.engines(other, core)))
        s, k = number[i]
        total[s] = max(total.get(s, 0), k)
    known = {e: {} for e in queues}
    after = {}

    def learn(a, b):
        for s, k in b.items():
            if a.get(s, 0) < k:
                a[s] = k
    emitted = {}
    pending = {e: list(queues[e]) for e in queues}
    while any(pending.values()):
        for e in pending:
            while pending[e]:
                i = pending[e][0]
                o = ops[i]
                if any(j not in emitted and ops[j]["kind"] != "arr" for j in o["deps"]):
                    break
                need = {}
                for j, raw in o["deps"].items():
                    if place[j] == e and ops[j]["kind"] == "c" and (e == "p" or not raw):
                        continue
                    s, k = number[j]
                    need[s] = max(need.get(s, 0), k)
                kn = known[e]
                todo = [(s, k) for s, k in need.items() if kn.get(s, 0) < k]
                for s, k in todo:
                    if any((s2, k2) != (s, k) and after.get((s2, k2), {}).get(s, 0) >= k for s2, k2 in todo):
                        continue
                    Q[e].wait_ge(T.sem[s], k)
                    learn(kn, {s: k})
                    learn(kn, after.get((s, k), {}))
                ins = o["fn"](Q[e], {"T": T, "topo": topo, "core": core, "rank": rank, "e": e})
                s, k = number[i]
                if o["kind"] == "c":
                    ins.then_inc(T.sem[s], 1)
                after[(s, k)] = dict(kn)
                emitted[i] = True
                pending[e].pop(0)
    for s in sorted(total):
        if known["g"].get(s, 0) < total[s]:
            g.wait_ge(T.sem[s], total[s])
